import numpy as np, ml_dtypes
CORES = [6,15,38,47]
N = 4
import mx_ref
BF = ml_dtypes.bfloat16
def entries(a):
    return np.ascontiguousarray(a.T).reshape(-1)
def table(e):
    return np.ascontiguousarray(np.reshape(e, (-1, 16)).T).astype(np.int32)
def cols(t, e):
    v = np.concatenate([t.reshape(128, -1, 4), np.zeros((128, 1, 4), BF)], axis=1)
    return np.ascontiguousarray(v[:, e]).reshape(128, -1)
def tile(rs):
    return np.stack(rs, axis=2).reshape(128, -1).astype(BF)
def cut(t, i, w=512):
    return t[:, w * i:w * i + w]
def f(rng, *shape):
    return mx_ref.flush((rng.standard_normal(shape, dtype=np.float32) * np.exp2(rng.integers(-2, 3, shape[:-1] + (1,)))).astype(BF))
def wide(rng, *shape, cols=0):
    v = rng.standard_normal(shape, dtype=np.float32) * np.exp2(rng.integers(-12, 13, shape)).astype(np.float32)
    if cols: v *= np.repeat(np.exp2(rng.integers(-cols, cols + 1, shape[:-2] + (1, shape[-1] // 4))) * (rng.random(shape[:-2] + (1, shape[-1] // 4)) > 0.0625), 4, axis=-1).astype(np.float32)
    return mx_ref.flush(v.astype(BF))
T, E, CN, CM = 256, 512, 128, 144
def lists(rng, popular=False, lonely=False, far=False):
    n, m = np.full((N, N, CN), -1), np.full((N, N, CM), -1)
    for q in range(N):
        for d in range(N):
            if d != q:
                k = rng.permutation(CN)[:CN if far else rng.integers(CN // 2, CN + 1)]; n[q, d, k] = rng.integers(0, T, len(k))
            k = rng.permutation(CM)[:CM if far else rng.integers(CM // 2, CM + 1)]; m[q, d, k] = 0
        u = m[q] == 0
        m[q][u] = rng.permutation(np.resize(rng.permutation(E), int(u.sum())))
    es, ed, nl = [], [], []
    for r in range(N):
        u = T + np.flatnonzero(n[:, r].reshape(-1) >= 0)
        if far: h = rng.permutation(np.resize(rng.permutation(u), 2 * E))
        else: h = rng.choice(np.concatenate([np.arange(T), u]), 2 * E)
        a, b = h[:E].copy(), h[E:].copy()
        if popular: a[rng.permutation(E)[:3 * E // 4]] = rng.choice(u)
        es.append(table(a)); ed.append(table(b))
        w = np.flatnonzero(m[:, r].reshape(-1) >= 0)
        j = rng.permutation(T)[:T // 2 if lonely else T]
        p = (4 * j[:, None] + rng.permuted(np.tile(np.arange(4), (len(j), 1)), axis=1)).T.reshape(-1)
        if not lonely: p = rng.permutation(p)
        k = len(p) if far else min(len(p), len(w) + int(rng.integers(0, T)))
        t = np.full(4 * T, -1); t[p[:k]] = rng.permutation(np.resize(rng.permutation(w), k))
        nl.append(table(t))
    return {"sn": np.stack([table(n[q].reshape(-1)) for q in range(N)]), "es": np.stack(es), "ed": np.stack(ed), "sm": np.stack([table(m[q].reshape(-1)) for q in range(N)]), "nl": np.stack(nl)}
def setup_inputs(rng):
    return {"x": f(rng, N, 128, 4 * T), "e": f(rng, N, 128, 4 * E), "wa": np.repeat(f(rng, 1, 128, 2048), N, axis=0), "wb": np.repeat(f(rng, 1, 128, 2048), N, axis=0), "v": f(rng, N, 128, 512), **lists(rng)}
def setup_inputs_popular(rng):
    return {**setup_inputs(rng), **lists(rng, popular=True)}
def setup_inputs_lonely(rng):
    d = {**setup_inputs(rng), **lists(rng, lonely=True)}; d["v"] = (d["v"].astype(np.float32) * np.float32(2.0 ** 24)).astype(BF); d["e"] = (d["e"].astype(np.float32) * np.float32(2.0 ** 20)).astype(BF); return d
def setup_inputs_far(rng):
    return {**setup_inputs(rng), **lists(rng, far=True)}
def setup_inputs_cancel(rng):
    d = setup_inputs(rng); d["wb"] = -d["wa"]
    for r in range(N):
        a, b = entries(d["es"][r]), entries(d["ed"][r]).copy()
        k = rng.permutation(E)[:3 * E // 4]; b[k] = a[k]; d["ed"][r] = table(b)
    d["e"] = mx_ref.flush((d["e"].astype(np.float32) * np.float32(2.0 ** -10)).astype(BF)); return d
def setup_inputs_spread(rng):
    d = setup_inputs(rng); d["x"] = wide(rng, N, 128, 4 * T, cols=4); d["e"] = wide(rng, N, 128, 4 * E, cols=4); return d
def check_inputs(d):
    b = []
    for k in ("wa", "wb"):
        if (d[k] != d[k][:1]).any(): b.append(k)
    n = [entries(d["sn"][q]).reshape(N, CN) for q in range(N)]; m = [entries(d["sm"][q]).reshape(N, CM) for q in range(N)]
    for r in range(N):
        if n[r].min() < -1 or n[r].max() >= T or (n[r][r] != -1).any(): b.append("sn")
        if m[r].min() < -1 or m[r].max() >= E: b.append("sm")
        ok = np.concatenate([np.ones(T, bool)] + [n[q][r] >= 0 for q in range(N)])
        for k in ("es", "ed"):
            h = entries(d[k][r])
            if h.min() < 0 or h.max() >= T + N * CN or not ok[h].all(): b.append(k)
        ok = np.concatenate([m[q][r] >= 0 for q in range(N)]); h = entries(d["nl"][r])
        if h.min() < -1 or h.max() >= N * CM or not ok[h[h >= 0]].all(): b.append("nl")
    return b
def reference(x, e, wa, wb, v, sn, es, ed, sm, nl):
    M = []
    for r in range(N):
        X = np.concatenate([x[r]] + [cols(x[q], entries(sn[q])[r * CN:r * CN + CN]) for q in range(N)], axis=1)
        src, dst = mx_ref.quantize(cols(X, entries(es[r]))), mx_ref.quantize(cols(X, entries(ed[r])))
        rs = []
        for i in range(4):
            a = mx_ref.matmul(mx_ref.quantize(np.ascontiguousarray(cut(wa[r], i))), src)
            b = mx_ref.matmul(mx_ref.quantize(np.ascontiguousarray(cut(wb[r], i))), dst)
            rs.append(np.maximum((a + b) + e[r][:, i::4].astype(np.float32), np.float32(0)) * np.float32(0.05))
        M.append(tile(rs))
    y = np.zeros((N, 128, T), np.float32)
    for r in range(N):
        P = mx_ref.matmul(mx_ref.quantize(v[r]), mx_ref.quantize(np.concatenate([cols(M[q], entries(sm[q])[r * CM:r * CM + CM]) for q in range(N)], axis=1)))
        k = entries(nl[r]).reshape(T, 4)
        z = np.where(k >= 0, P[:, k], np.float32(-np.inf)).max(axis=2)
        y[r] = np.where((k >= 0).any(axis=1), z, np.float32(0))
    return {"y": y}

@@ -1,0 +1,368 @@
+from concourse.mybir import dt, AluOpType, ActivationFunctionType
+from concourse.bass import IndirectOffsetOnAxis
+
+N, NT, E, CN, CM = 4, 256, 512, 128, 144
+NH = NT + N * CN
+XO = 16
+WO = 8
+NA = 64
+ALU, ACT = AluOpType, ActivationFunctionType
+OWN = "ssssssss"
+LATE = ["ssssssss", "ssssssss", "vvssvvss"]
+
+SCRATCH = {
+    "xb": ("sbuf", [128, XO + 4 * NT], "bfloat16"),
+    "eb": ("sbuf", [128, XO + 4 * E], "bfloat16"),
+    "wab": ("sbuf", [128, 2048], "bfloat16"),
+    "wbb": ("sbuf", [128, 2048], "bfloat16"),
+    "vb": ("sbuf", [128, 512], "bfloat16"),
+    "ht": ("sbuf", [128, 4 * 3 * CN], "bfloat16"),
+    "mt": ("sbuf", [128, 4 * N * CM], "bfloat16"),
+    "pa": ("sbuf", [128, 4 * NH], "float32"),
+    "pb": ("sbuf", [128, 4 * NH], "float32"),
+    "nld": ("dram", [4, 256], "int32"),
+    "ps": ("psum", [128, 4096], "float32"),
+}
+for _n, _w in (("snl", 32), ("sml", 36), ("eds", 64), ("nlr", 256), ("pi", 1), ("b4i", 1), ("i4i", 1), ("ci", 144), ("co", 288)):
+    SCRATCH[_n] = ("sbuf", [128, _w], "int32")
+for _n, _w in (("pk1", 32), ("pk2", 32), ("pk", 32), ("pkt", 32), ("prow", 512), ("wn", 512), ("b4f", 1), ("ic", 1), ("ipk", 1),
+               ("jm", 576), ("kk", 512), ("mask", 576), ("carry", 576), ("mv", 576), ("sc", 576), ("mv2", 576), ("sc2", 576),
+               ("nmv", 256), ("nsc", 256), ("nt1", 32), ("nt2", 16), ("nt3", 16), ("nt4", 16), ("win", WO + N * CM),
+               ("g0", NT), ("m1", NT), ("m2", NT), ("yb", NT)):
+    SCRATCH[_n] = ("sbuf", [128, _w], "float32")
+for _n, _w in (("smo", 36), ("oe", 144), ("oab", 288), ("onl", 64), ("oft0", 32), ("oft1", 32), ("oft2", 32), ("oft3", 32)):
+    SCRATCH[_n] = ("sbuf", [128, _w], "uint16")
+for _k in range(4):
+    for _n in ("gb", "uu", "zz"):
+        SCRATCH["%s%d" % (_n, _k)] = ("sbuf", [128, 4 * CM], "float32")
+for _n, _w in (("h", 3 * CN), ("nn", N * CN), ("xx", NT), ("wa", 512), ("wb", 512), ("vv", 128), ("mm", N * CM), ("rr", N * CM)):
+    SCRATCH[_n + "q"] = ("sbuf", [128, _w], "float8_e4m3fn_x4")
+    SCRATCH[_n + "p"] = ("sbuf", [128, _w], "uint8")
+
+SEMAPHORES = ["cv", "cs", "ct", "cg", "d_ed", "d_sn", "d_x", "d_wa", "d_wb", "d_sm", "d_nl", "d_pr", "d_e", "d_v", "d_g", "d_y",
+              "lno", "lme", "go"] + ["an%d" % _k for _k in range(4)] + ["am%d" % _k for _k in range(4)]
+
+
+def rank_program(g, core, T, topo):
+    r = T.rank_of(core)
+    if r is None:
+        return
+    S = T.sem
+    Q = {"g": g, "v": g.vector, "s": g.scalar, "t": g.tensor, "y": g.sync}
+    CS = {"v": "cv", "s": "cs", "t": "ct", "g": "cg"}
+    V, A, PE = g.vector, g.scalar, g.tensor
+    seen, cnt = {}, {}
+
+    def need(q, *toks):
+        best = {}
+        for k, n in toks:
+            best[k] = max(best.get(k, 0), n)
+        for k in best:
+            if seen.get((q, k), 0) < best[k]:
+                Q[q].wait_ge(S[k], best[k])
+                seen[(q, k)] = best[k]
+
+    def did(q, ins):
+        k = CS[q]
+        cnt[k] = cnt.get(k, 0) + 1
+        ins.then_inc(S[k], 1)
+        return (k, cnt[k])
+
+    def dma(q, sem, out, in_):
+        Q[q].dma_start(out, in_).then_inc(S[sem], 16)
+        cnt[sem] = cnt.get(sem, 0) + 16
+
+    def tok(sem):
+        return (sem, cnt[sem])
+
+    def ts(out, in0, s1, op, s2=None, op2=None):
+        if op2 is None:
+            return did("v", V.tensor_scalar(out, in0, s1, None, op))
+        return did("v", V.tensor_scalar(out, in0, s1, s2, op, op2))
+
+    def tt(out, in0, in1, op):
+        return did("v", V.tensor_tensor(out, in0, in1, op))
+
+    def copy(q, out, in_):
+        return did(q, V.tensor_copy(out, in_) if q == "v" else A.activation(out, in_, ACT.Copy))
+
+    def near(d):
+        a, b = topo.chip(core), topo.chip(T.cores[d])
+        return 2 if topo.mates(a, b) else 1 if topo.same_plane(a, b) else 0
+    others = sorted([d for d in range(N) if d != r], key=near)
+    blocks = others + [r]
+
+    def send(d, lsem, pairs, rsem):
+        dst = T.cores[d]
+        rid, pid, _ = topo.addr(dst)
+        for o, i in pairs:
+            g.remote_dma(o, i, S[rsem], S[lsem], pid, rid, topo.mask(core, dst))
+            cnt[lsem] = cnt.get(lsem, 0) + len(topo.engines(core, dst))
+
+    def arrived(s):
+        return 2 * len(topo.engines(T.cores[s], core))
+
+    dma("y", "d_ed", T.eds[0:16, 0:32], T.es[:, :])
+    dma("y", "d_ed", T.eds[0:16, 32:64], T.ed[:, :])
+    for k in range(8):
+        dma("y" if k < 3 else "s", "d_sn", T.snl[16 * k:16 * k + 16, :], T.sn[:, :])
+    dma("y", "d_x", T.xb[:, XO:XO + 512], T.x[:, 0:512])
+    dma("s", "d_x", T.xb[:, XO + 512:XO + 1024], T.x[:, 512:1024])
+    dma("s", "d_wa", T.wab[:, :], T.wa[:, :])
+    for k in range(8):
+        dma("y", "d_sm", T.sml[16 * k:16 * k + 16, :], T.sm[:, :])
+
+    k_pi = did("g", g.iota(T.pi[:, :], [[0, 1]], 0, 1))
+    k_jm = did("g", g.iota(T.jm[:, :], [[0, 144], [1, 4]], 0, 0, allow_small_or_imprecise_dtypes=True))
+    k_kk = did("g", g.iota(T.kk[:, :], [[1, 512]], 0, 0, allow_small_or_imprecise_dtypes=True))
+    did("v", V.memset(T.pk[0:32, :], 0.0))
+    k_c = did("v", V.memset(T.carry[:, :], 1.0))
+    k_xb = did("v", V.memset(T.xb[:, 0:XO], 0.0))
+    k_eb = did("v", V.memset(T.eb[:, 0:XO], 0.0))
+    did("v", V.memset(T.win[:, 0:WO - 1], 0.0))
+    k_win = did("v", V.memset(T.win[:, WO - 1:WO], -1e29))
+    need("v", k_c)
+    k_c = did("v", V.memset(T.carry[:, 0:576:4], 0.0))
+    need("v", k_pi)
+    ts(T.b4i[:, :], T.pi[:, :], 2, ALU.logical_shift_right, 3, ALU.bitwise_and)
+    k_i4 = ts(T.i4i[:, :], T.pi[:, :], 3, ALU.bitwise_and)
+    need("v", k_i4)
+    k_bf = copy("v", T.b4f[:, :], T.b4i[:, :])
+    k_ic = ts(T.ic[:, :], T.i4i[:, :], float(XO), ALU.add)
+    k_ip = ts(T.ipk[:, :], T.i4i[:, :], 4097.0, ALU.mult)
+    need("v", k_jm, k_bf)
+    k_mask = ts(T.mask[:, :], T.jm[:, :], T.b4f[:, 0:1], ALU.is_equal)
+    hole = 4 * (NT + CN * r)
+    need("s", k_c)
+    did("s", A.activation(T.pa[:, hole:hole + 4 * CN], T.carry[:, 0:512], ACT.Copy, scale=0.0))
+    k_hole = did("s", A.activation(T.pb[:, hole:hole + 4 * CN], T.carry[:, 0:512], ACT.Copy, scale=0.0))
+
+    need("v", tok("d_ed"))
+    ts(T.pk1[0:16, :], T.eds[0:16, 0:32], 4.0, ALU.mult)
+    k = ts(T.pk2[0:16, :], T.eds[0:16, 32:64], 16384.0, ALU.mult)
+    need("v", tok("d_sn"))
+    k_of = {}
+    for t in (2, 3, 0, 1):
+        k_of[t] = ts(T["oft%d" % t][:, :], T.snl[:, :], 4.0, ALU.mult, float(XO + t), ALU.add)
+    need("v", k)
+    k = tt(T.pk[0:16, :], T.pk1[0:16, :], T.pk2[0:16, :], ALU.add)
+    need("v", k)
+    k_pkt = did("v", V.transpose(T.pkt[0:32, :], T.pk[0:32, :]))
+    need("y", k_pkt)
+    dma("y", "d_pr", T.prow[0:1, :], T.pkt[0:32, 0:16])
+    dma("y", "d_wb", T.wbb[:, :], T.wb[:, :])
+    dma("y", "d_nl", T.nld[:, :], T.nl[:, :])
+
+    need("v", tok("d_x"), k_xb)
+    need("s", tok("d_x"), k_xb)
+    for o, d in enumerate(others):
+        ks = []
+        for q, t in (("v", 0), ("v", 1), ("s", 2), ("s", 3)):
+            need(q, k_of[t])
+            ks.append(copy(q, T.ht[:, 512 * o + t:512 * o + 512:4], T.xb[:, :].indirect(T["oft%d" % t][:, 8 * d:8 * d + 8])))
+        need("v", *ks)
+        here, there = slice(CN * o, CN * o + CN), slice(CN * r, CN * r + CN)
+        k = did("v", V.quantize_mx(T.hq[:, here], T.hp[:, here], T.ht[:, 512 * o:512 * o + 512]))
+        need("g", k)
+        send(d, "lno", [(T.nnq[:, there].bitcast(dt.uint8), T.hq[:, here].bitcast(dt.uint8)), (T.nnp[:, there], T.hp[:, here])], "an%d" % r)
+    g.sem_inc(S.go, 1)
+    cnt["go"] = 1
+    need("y", tok("go"))
+    dma("y", "d_e", T.eb[:, XO:XO + 4 * E], T.e[:, :])
+    dma("y", "d_v", T.vb[:, :], T.v[:, :])
+    need("g", tok("d_pr"))
+    k_wn = did("g", g.partition_broadcast(T.wn[:, :], T.prow[0:1, :], 128))
+    need("g", tok("d_nl"), k_i4)
+    g.indirect_dma_start(T.nlr[:, :], None, T.nld[:, :], IndirectOffsetOnAxis(ap=T.i4i[:, 0:1], axis=0), bounds_check=3).then_inc(S.d_g, 16)
+    cnt["d_g"] = 16
+
+    need("v", tok("d_wa"))
+    k_wq = did("v", V.quantize_mx(T.waq[:, :], T.wap[:, :], T.wab[:, :]))
+    k_xq = did("v", V.quantize_mx(T.xxq[:, :], T.xxp[:, :], T.xb[:, XO:XO + 1024]))
+    need("v", tok("d_wb"))
+    k_uq = did("v", V.quantize_mx(T.wbq[:, :], T.wbp[:, :], T.wbb[:, :]))
+
+    bank = [None] * 8
+    k_pw = []
+
+    def products(cq, cp, n, who):
+        ks = {}
+        for j in who:
+            c, p = (T.waq, T.wap) if j < 4 else (T.wbq, T.wbp)
+            b = slice(128 * (j % 4), 128 * (j % 4) + 128)
+            need("t", k_wq if j < 4 else k_uq)
+            if bank[j]:
+                need("t", bank[j])
+            ks[j] = did("t", PE.matmul_mx(T.ps[:, 512 * j:512 * j + n], c[:, b], p[:, b], cq, cp, True, True))
+        return ks
+
+    def take(q, plan, h, n, ks):
+        for j in ks:
+            if plan[j] == q:
+                need(q, ks[j])
+                bank[j] = copy(q, (T.pa if j < 4 else T.pb)[:, 4 * h + j % 4:4 * h + 4 * n:4], T.ps[:, 512 * j:512 * j + n])
+                k_pw.append(bank[j])
+
+    need("t", k_xq)
+    own = (OWN, 0, NT, products(T.xxq[:, :], T.xxp[:, :], NT, range(8)))
+    take("s", *own)
+
+    need("v", tok("d_sm"))
+    k_smo = ts(T.smo[:, :], T.sml[:, :], 0.0, ALU.max)
+    need("v", k_smo, k_kk, k_mask)
+    k = tt(T.mv2[:, :], T.kk[:, :].indirect(T.smo[:, :]), T.mask[:, :], ALU.mult)
+    need("v", k, k_c)
+    k = did("v", V.tensor_tensor_scan(T.sc2[:, :], T.carry[:, :], T.mv2[:, :], 0.0, ALU.mult, ALU.add))
+    take("v", *own)
+    need("v", k, k_ic)
+    k_oe = ts(T.oe[:, :], T.sc2[:, 3:576:4], 4.0, ALU.mult, T.ic[:, 0:1], ALU.add)
+
+    def late(o):
+        s = others[o]
+        b = slice(CN * s, CN * s + CN)
+        need("t", ("an%d" % s, arrived(s)))
+        return LATE[o], NT + CN * s, CN, products(T.nnq[:, b], T.nnp[:, b], CN, (4, 5, 6, 7, 0, 1, 2, 3))
+
+    la = late(0)
+    take("s", *la)
+    need("v", k_wn)
+    k = tt(T.mv[:, :], T.wn[:, :].indirect(T.smo[:, :]), T.mask[:, :], ALU.mult)
+    need("v", k)
+    k = did("v", V.tensor_tensor_scan(T.sc[:, :], T.carry[:, :], T.mv[:, :], 0.0, ALU.mult, ALU.add))
+    take("v", *la)
+    need("v", k, k_ip)
+    k = ts(T.ci[:, :], T.sc[:, 3:576:4], T.ipk[:, 0:1], ALU.add)
+    lb = late(1)
+    take("s", *lb)
+    need("v", k)
+    kh = ts(T.co[:, 144:288], T.ci[:, :], 12, ALU.logical_shift_right)
+    kl = ts(T.co[:, 0:144], T.ci[:, :], 4095, ALU.bitwise_and)
+    take("v", *lb)
+    need("v", kh)
+    k_ob = copy("v", T.oab[:, 144:288], T.co[:, 144:288])
+    need("v", kl)
+    k_oa = copy("v", T.oab[:, 0:144], T.co[:, 0:144])
+    lc = late(2)
+    take("v", *lc)
+    take("s", *lc)
+
+    W, H = 4 * CM, 2 * CM
+    gb, uu, zz = ([T["%s%d" % (n, o)] for o in range(4)] for n in ("gb", "uu", "zz"))
+    k_gb, k_u, k_z, k_r, k_q = {}, {}, {}, {}, {}
+
+    def list_of(t, base, o, a=0, n=36):
+        c = base + 36 * blocks[o] + a
+        return t[:, c:c + n]
+
+    def gather_b(q, o, a=0, b=W):
+        need(q, *k_pw, k_hole, k_ob)
+        k_gb.setdefault(o, []).append(copy(q, gb[o][:, a:b], T.pb[:, :].indirect(list_of(T.oab, 144, o, a // 16, (b - a) // 16))))
+
+    def add_a(o):
+        need("v", *k_pw, k_hole, k_oa, *k_gb[o])
+        k_u[o] = tt(uu[o][:, :], T.pa[:, :].indirect(list_of(T.oab, 0, o)), gb[o][:, :], ALU.add)
+
+    def add_e(o):
+        need("v", tok("d_e"), k_eb, k_oe, k_u[o])
+        k_z[o] = tt(zz[o][:, :], T.eb[:, :].indirect(list_of(T.oe, 0, o)), uu[o][:, :], ALU.add)
+
+    def relu(q, o, a, b):
+        need(q, k_z[o])
+        out = T.mt[:, W * o + a:W * o + b]
+        if q == "s":
+            k = did("s", A.activation(out, zz[o][:, a:b], ACT.Relu, scale=0.05))
+        else:
+            k = ts(out, zz[o][:, a:b], 0.0, ALU.max, 0.05, ALU.mult)
+        k_r.setdefault(o, []).append(k)
+
+    def quant(o):
+        need("v", *k_r[o])
+        here, there = slice(CM * o, CM * o + CM), slice(CM * r, CM * r + CM)
+        k_q[o] = did("v", V.quantize_mx(T.mmq[:, here], T.mmp[:, here], T.mt[:, W * o:W * o + W]))
+        if blocks[o] != r:
+            need("g", k_q[o])
+            send(blocks[o], "lme", [(T.rrq[:, there].bitcast(dt.uint8), T.mmq[:, here].bitcast(dt.uint8)), (T.rrp[:, there], T.mmp[:, here])], "am%d" % r)
+
+    gather_b("s", 0, 0, H)
+    gather_b("v", 0, H, W)
+    gather_b("s", 1)
+    gather_b("s", 2)
+    add_a(0)
+    add_e(0)
+    relu("s", 0, 0, W)
+    add_a(1)
+    gather_b("s", 3)
+    add_e(1)
+    quant(0)
+    relu("s", 1, 0, W)
+    add_a(2)
+    quant(1)
+    add_e(2)
+    relu("s", 2, 0, H)
+    relu("v", 2, H, W)
+    quant(2)
+    add_a(3)
+    need("v", tok("d_g"))
+    k = tt(T.nmv[:, :], T.nlr[:, :], T.mask[:, 0:256], ALU.mult)
+    need("v", tok("d_v"))
+    k_vq = did("v", V.quantize_mx(T.vvq[:, :], T.vvp[:, :], T.vb[:, :]))
+    add_e(3)
+    need("v", k)
+    k = did("v", V.tensor_tensor_scan(T.nsc[:, :], T.carry[:, 0:256], T.nmv[:, :], 0.0, ALU.mult, ALU.add))
+    relu("s", 3, 0, H)
+    relu("v", 3, H, W)
+    need("v", k)
+    k = tt(T.nt1[:, :], T.nsc[:, 3:128:4], T.nsc[:, 131:256:4], ALU.max)
+    quant(3)
+    need("v", k)
+    k = tt(T.nt2[:, :], T.nt1[:, 0:16], T.nt1[:, 16:32], ALU.max)
+    ts(T.onl[:, 16:64], T.nsc[:, 67:256:4], float(WO), ALU.add)
+    need("v", k)
+    k = ts(T.nt3[:, :], T.nt2[:, :], 0.0, ALU.is_lt)
+    need("v", k)
+    k = tt(T.nt4[:, :], T.nsc[:, 3:64:4], T.nt3[:, :], ALU.subtract)
+    need("v", k)
+    k_onl = ts(T.onl[:, 0:16], T.nt4[:, :], float(WO), ALU.add)
+
+    need("t", k_vq)
+    k_w = []
+    for n, o in enumerate((0, 3, 1, 2)):
+        s = blocks[o]
+        if s == r:
+            need("t", k_q[o])
+            cq, cp = T.mmq[:, CM * o:CM * o + CM], T.mmp[:, CM * o:CM * o + CM]
+        else:
+            need("t", ("am%d" % s, arrived(s)))
+            cq, cp = T.rrq[:, CM * s:CM * s + CM], T.rrp[:, CM * s:CM * s + CM]
+        need("t", bank[n])
+        k = did("t", PE.matmul_mx(T.ps[:, 512 * n:512 * n + CM], T.vvq[:, :], T.vvp[:, :], cq, cp, True, True))
+        need("s", k)
+        k_w.append(copy("s", T.win[:, WO + CM * s:WO + CM * s + CM], T.ps[:, 512 * n:512 * n + CM]))
+
+    def at(f, a, b):
+        return T.win[:, :].indirect(T.onl[:, 16 * f + a // 16:16 * f + b // 16])
+
+    def largest(f, a, b, k):
+        i, o = (None, (T.g0, T.m1), (T.m1, T.m2), (T.m2, T.yb))[f]
+        need("v", k)
+        return tt(o[:, a:b], at(f, a, b), i[:, a:b], ALU.max)
+
+    need("s", k_onl, k_win, *k_w)
+    need("v", k_onl, k_win, *k_w)
+    kb = copy("s", T.g0[:, NA:NT], at(0, NA, NT))
+    ka = copy("v", T.g0[:, 0:NA], at(0, 0, NA))
+    ka = largest(1, 0, NA, ka)
+    ka = largest(2, 0, NA, ka)
+    kb = largest(1, NA, NT, kb)
+    ka = largest(3, 0, NA, ka)
+    kb = largest(2, NA, NT, kb)
+    kb = largest(3, NA, NT, kb)
+    need("y", ka)
+    dma("y", "d_y", T.y[:, 0:NA], T.yb[:, 0:NA])
+    need("y", kb)
+    dma("y", "d_y", T.y[:, NA:NT], T.yb[:, NA:NT])
+
+    for k in cnt:
+        need("g", tok(k))
+    for s in others:
+        need("g", ("an%d" % s, arrived(s)), ("am%d" % s, arrived(s)))

@@ -3,16 +3,15 @@ from concourse.bass import IndirectOffsetOnAxis
 
 N, NT, E, CN, CM = 4, 256, 512, 128, 144
 NH = NT + N * CN
-XO = 16
 WO = 8
 NA = 64
+W, H = 4 * CM, 2 * CM
+UP = 2.0 ** 24
 ALU, ACT = AluOpType, ActivationFunctionType
-OWN = "ssssssss"
-LATE = ["ssssssss", "ssssssss", "vvssvvss"]
 
 SCRATCH = {
-    "xb": ("sbuf", [128, XO + 4 * NT], "bfloat16"),
-    "eb": ("sbuf", [128, XO + 4 * E], "bfloat16"),
+    "xb": ("sbuf", [128, 4 * NT], "bfloat16"),
+    "eb": ("sbuf", [128, 4 * E], "bfloat16"),
     "wab": ("sbuf", [128, 2048], "bfloat16"),
     "wbb": ("sbuf", [128, 2048], "bfloat16"),
     "vb": ("sbuf", [128, 512], "bfloat16"),
@@ -21,26 +20,47 @@ SCRATCH = {
     "pa": ("sbuf", [128, 4 * NH], "float32"),
     "pb": ("sbuf", [128, 4 * NH], "float32"),
     "nld": ("dram", [4, 256], "int32"),
+    "smd": ("dram", [4, 144], "int32"),
     "ps": ("psum", [128, 4096], "float32"),
 }
-for _n, _w in (("snl", 32), ("sml", 36), ("eds", 64), ("nlr", 256), ("pi", 1), ("b4i", 1), ("i4i", 1), ("ci", 144), ("co", 288)):
+for _n, _w in (("snl", 32), ("sml", 36), ("eds", 256), ("nlr", 256), ("smr", 144), ("pi", 1), ("ai", 1), ("ii", 1), ("ci", 144), ("cl", 144),
+               ("k0", 36), ("k1", 36), ("k2", 36), ("k3", 36)):
     SCRATCH[_n] = ("sbuf", [128, _w], "int32")
-for _n, _w in (("pk1", 32), ("pk2", 32), ("pk", 32), ("pkt", 32), ("prow", 512), ("wn", 512), ("b4f", 1), ("ic", 1), ("ipk", 1),
-               ("jm", 576), ("kk", 512), ("mask", 576), ("carry", 576), ("mv", 576), ("sc", 576), ("mv2", 576), ("sc2", 576),
-               ("nmv", 256), ("nsc", 256), ("nt1", 32), ("nt2", 16), ("nt3", 16), ("nt4", 16), ("win", WO + N * CM),
-               ("g0", NT), ("m1", NT), ("m2", NT), ("yb", NT)):
+for _n, _w in (("pk1", 128), ("pk", 128), ("wn", 512), ("af", 1), ("ic", 1), ("ic4", 1), ("j4", 4), ("w1", 4), ("w2", 4),
+               ("w4", 4), ("one", CM), ("wt", W), ("gg", W), ("sc", W), ("nmv", 256), ("nsc", 256), ("nt1", 32), ("nt2", 16), ("nt3", 16),
+               ("nt4", 16), ("win", WO + N * CM), ("g0", NT), ("m1", NT), ("m2", NT), ("yb", NT)):
     SCRATCH[_n] = ("sbuf", [128, _w], "float32")
-for _n, _w in (("smo", 36), ("oe", 144), ("oab", 288), ("onl", 64), ("oft0", 32), ("oft1", 32), ("oft2", 32), ("oft3", 32)):
+for _n, _w in (("smo", 36), ("oe", 144), ("oa", 144), ("ob", 144), ("onl", 64), ("oft0", 32), ("oft1", 32), ("oft2", 32), ("oft3", 32)):
     SCRATCH[_n] = ("sbuf", [128, _w], "uint16")
 for _k in range(4):
     for _n in ("gb", "uu", "zz"):
-        SCRATCH["%s%d" % (_n, _k)] = ("sbuf", [128, 4 * CM], "float32")
+        SCRATCH["%s%d" % (_n, _k)] = ("sbuf", [128, W], "float32")
 for _n, _w in (("h", 3 * CN), ("nn", N * CN), ("xx", NT), ("wa", 512), ("wb", 512), ("vv", 128), ("mm", N * CM), ("rr", N * CM)):
     SCRATCH[_n + "q"] = ("sbuf", [128, _w], "float8_e4m3fn_x4")
     SCRATCH[_n + "p"] = ("sbuf", [128, _w], "uint8")
 
-SEMAPHORES = ["cv", "cs", "ct", "cg", "d_ed", "d_sn", "d_x", "d_wa", "d_wb", "d_sm", "d_nl", "d_pr", "d_e", "d_v", "d_g", "d_y",
-              "lno", "lme", "go"] + ["an%d" % _k for _k in range(4)] + ["am%d" % _k for _k in range(4)]
+LOADS = ["sn", "x", "ed", "wa", "wb", "sm", "smd", "nld", "e", "v", "smr", "nlr", "y"]
+SEMAPHORES = ["cv", "cs", "ct", "cg", "lno", "lme", "go"] + ["d_" + _n for _n in LOADS] + ["an%d" % _k for _k in range(4)] + ["am%d" % _k for _k in range(4)]
+
+
+def seq(name, items):
+    return [name + str(i) for i in items]
+
+
+ORDER = {
+    "y": "sn.0 x.0 ed.0 sm.0 smd.0 smd.1 nld.0 wb.0 e.0 v.0 y.0 y.1",
+    "s": "sn.1 x.1 ed.1 sm.1 smd.2 smd.3 wa.0 wt0 wt1 wt2 wt3 "
+         "n02 n03 n12 n13 n11 n22 n23 n21 holeb oC0 oC1 oC2 oC3 G oC6 fC4 fC1 fC0 fC6 fC2 mC4 mC6 mC1 mC0 mC2 B0a "
+         "B1 B2 R0 B3 R1 R2a R3a R3b vC0 vC1 vC3 vC2 y0b",
+    "v": "ed0 ai one af ii w1 w2 ic w4 ic4 w3 sn1 win0 sn2 win1 of2 of3 of0 of1 "
+         "n00 n01 pk1 hq0 n10 pk hq1 n20 k0 k1 qx k2 hq2 k3 qa smo sm1 sm2 qb "
+         "oC4 oC5 oC7 scan fC5 ci ob cl fC7 oa fC3 mC5 mC7 mC3 B0b oe0 oe1 oe2 oe3 "
+         "A0 A1 E0 A2 E1 Q0 E2 Q1 nl1 R2b qv Q2 A3 nl2 E3 nl3 nl5 nl4 nl6 nl7 Q3 nl8 "
+         "y0a y1a y1b y2a y2b y3a y3b",
+    "t": "oP0 oP1 oP2 oP3 oP4 oP5 oP7 oP6 fP4 fP5 fP1 fP0 fP7 fP6 fP3 fP2 mP5 mP4 mP7 mP6 mP1 mP0 mP3 mP2 vP0 vP1 vP3 vP2",
+    "g": "pi j4 holea sn0 wn0 sn1s sn2s go wn1 wn2 wn3 smr.0 nlr.0 sm0s sm1s sm2s",
+}
+ORDER = {_q: ORDER[_q].split() for _q in ORDER}
 
 
 def rank_program(g, core, T, topo):
@@ -49,320 +69,226 @@ def rank_program(g, core, T, topo):
         return
     S = T.sem
     Q = {"g": g, "v": g.vector, "s": g.scalar, "t": g.tensor, "y": g.sync}
-    CS = {"v": "cv", "s": "cs", "t": "ct", "g": "cg"}
     V, A, PE = g.vector, g.scalar, g.tensor
-    seen, cnt = {}, {}
-
-    def need(q, *toks):
-        best = {}
-        for k, n in toks:
-            best[k] = max(best.get(k, 0), n)
-        for k in best:
-            if seen.get((q, k), 0) < best[k]:
-                Q[q].wait_ge(S[k], best[k])
-                seen[(q, k)] = best[k]
-
-    def did(q, ins):
-        k = CS[q]
-        cnt[k] = cnt.get(k, 0) + 1
-        ins.then_inc(S[k], 1)
-        return (k, cnt[k])
-
-    def dma(q, sem, out, in_):
-        Q[q].dma_start(out, in_).then_inc(S[sem], 16)
-        cnt[sem] = cnt.get(sem, 0) + 16
-
-    def tok(sem):
-        return (sem, cnt[sem])
-
-    def ts(out, in0, s1, op, s2=None, op2=None):
-        if op2 is None:
-            return did("v", V.tensor_scalar(out, in0, s1, None, op))
-        return did("v", V.tensor_scalar(out, in0, s1, s2, op, op2))
-
-    def tt(out, in0, in1, op):
-        return did("v", V.tensor_tensor(out, in0, in1, op))
-
-    def copy(q, out, in_):
-        return did(q, V.tensor_copy(out, in_) if q == "v" else A.activation(out, in_, ACT.Copy))
+    task = {}
+    tok = {}
 
     def near(d):
         a, b = topo.chip(core), topo.chip(T.cores[d])
         return 2 if topo.mates(a, b) else 1 if topo.same_plane(a, b) else 0
     others = sorted([d for d in range(N) if d != r], key=near)
     blocks = others + [r]
+    for s in others:
+        n = 2 * len(topo.engines(T.cores[s], core))
+        tok["an%d" % s], tok["am%d" % s] = ("an%d" % s, n), ("am%d" % s, n)
 
-    def send(d, lsem, pairs, rsem):
+    def add(name, deps, fn):
+        task[name] = (deps, fn)
+
+    def dma(name, deps, out, in_):
+        add(name, deps, lambda q: Q[q].dma_start(out, in_))
+
+    def ts(name, deps, out, in0, s1, op, s2=None, op2=None):
+        if op2 is None:
+            add(name, deps, lambda q: V.tensor_scalar(out, in0, s1, None, op))
+        else:
+            add(name, deps, lambda q: V.tensor_scalar(out, in0, s1, s2, op, op2))
+
+    def tt(name, deps, out, in0, in1, op):
+        add(name, deps, lambda q: V.tensor_tensor(out, in0, in1, op))
+
+    def copy(name, deps, out, in_):
+        add(name, deps, lambda q: V.tensor_copy(out, in_) if q == "v" else A.activation(out, in_, ACT.Copy))
+
+    def fill(name, out, c):
+        add(name, [], lambda q: V.memset(out, c) if q == "v" else g.iota(out, [[0, 4 * CN]], 0, 0, allow_small_or_imprecise_dtypes=True))
+
+    def quant(name, deps, c, p, in_):
+        add(name, deps, lambda q: V.quantize_mx(c, p, in_))
+
+    def pick(name, deps, out, in_, n):
+        add(name, deps + seq("wt", range(4)), lambda q: V.tensor_tensor_scan(out[:, :], in_[:, :], T.wt[:, 0:n], 0.0, ALU.max, ALU.mult))
+
+    sent = {"lno": 0, "lme": 0}
+
+    def send(name, deps, d, lsem, rsem, pairs):
         dst = T.cores[d]
         rid, pid, _ = topo.addr(dst)
-        for o, i in pairs:
-            g.remote_dma(o, i, S[rsem], S[lsem], pid, rid, topo.mask(core, dst))
-            cnt[lsem] = cnt.get(lsem, 0) + len(topo.engines(core, dst))
+        sent[lsem] += len(pairs) * len(topo.engines(core, dst))
 
-    def arrived(s):
-        return 2 * len(topo.engines(T.cores[s], core))
+        def fn(q):
+            for o, i in pairs:
+                g.remote_dma(o, i, S[rsem], S[lsem], pid, rid, topo.mask(core, dst))
+        add(name, deps, fn)
 
-    dma("y", "d_ed", T.eds[0:16, 0:32], T.es[:, :])
-    dma("y", "d_ed", T.eds[0:16, 32:64], T.ed[:, :])
-    for k in range(8):
-        dma("y" if k < 3 else "s", "d_sn", T.snl[16 * k:16 * k + 16, :], T.sn[:, :])
-    dma("y", "d_x", T.xb[:, XO:XO + 512], T.x[:, 0:512])
-    dma("s", "d_x", T.xb[:, XO + 512:XO + 1024], T.x[:, 512:1024])
-    dma("s", "d_wa", T.wab[:, :], T.wa[:, :])
-    for k in range(8):
-        dma("y", "d_sm", T.sml[16 * k:16 * k + 16, :], T.sm[:, :])
+    def spread(name, dep, t):
+        copy(name + "1", [dep], t[32:64, :], t[0:32, :])
+        copy(name + "2", [name + "1"], t[64:128, :], t[0:64, :])
 
-    k_pi = did("g", g.iota(T.pi[:, :], [[0, 1]], 0, 1))
-    k_jm = did("g", g.iota(T.jm[:, :], [[0, 144], [1, 4]], 0, 0, allow_small_or_imprecise_dtypes=True))
-    k_kk = did("g", g.iota(T.kk[:, :], [[1, 512]], 0, 0, allow_small_or_imprecise_dtypes=True))
-    did("v", V.memset(T.pk[0:32, :], 0.0))
-    k_c = did("v", V.memset(T.carry[:, :], 1.0))
-    k_xb = did("v", V.memset(T.xb[:, 0:XO], 0.0))
-    k_eb = did("v", V.memset(T.eb[:, 0:XO], 0.0))
-    did("v", V.memset(T.win[:, 0:WO - 1], 0.0))
-    k_win = did("v", V.memset(T.win[:, WO - 1:WO], -1e29))
-    need("v", k_c)
-    k_c = did("v", V.memset(T.carry[:, 0:576:4], 0.0))
-    need("v", k_pi)
-    ts(T.b4i[:, :], T.pi[:, :], 2, ALU.logical_shift_right, 3, ALU.bitwise_and)
-    k_i4 = ts(T.i4i[:, :], T.pi[:, :], 3, ALU.bitwise_and)
-    need("v", k_i4)
-    k_bf = copy("v", T.b4f[:, :], T.b4i[:, :])
-    k_ic = ts(T.ic[:, :], T.i4i[:, :], float(XO), ALU.add)
-    k_ip = ts(T.ipk[:, :], T.i4i[:, :], 4097.0, ALU.mult)
-    need("v", k_jm, k_bf)
-    k_mask = ts(T.mask[:, :], T.jm[:, :], T.b4f[:, 0:1], ALU.is_equal)
+    for k in range(2):
+        dma("sn.%d" % k, [], T.snl[16 * k:16 * k + 16, :], T.sn[:, :])
+        dma("sm.%d" % k, [], T.sml[16 * k:16 * k + 16, :], T.sm[:, :])
+        dma("x.%d" % k, [], T.xb[64 * k:64 * k + 64, :], T.x[64 * k:64 * k + 64, :])
+    fill("ed0", T.eds[:, :], 0)
+    dma("ed.0", ["ed0"], T.eds[0:128:32, 0:128], T.es[:, :])
+    dma("ed.1", ["ed0"], T.eds[0:128:32, 128:256], T.ed[:, :])
+    dma("wa.0", [], T.wab[:, :], T.wa[:, :])
+    dma("wb.0", [], T.wbb[:, :], T.wb[:, :])
+    for a in range(4):
+        dma("smd.%d" % a, [], T.smd[a:a + 1, :], T.sm[a:16:4, :])
+    dma("nld.0", [], T.nld[:, :], T.nl[:, :])
+    dma("e.0", ["go"], T.eb[:, :], T.e[:, :])
+    dma("v.0", [], T.vb[:, :], T.v[:, :])
+    add("go", [], lambda q: g.sem_inc(S.go, 1))
+    tok["go"] = ("go", 1)
+
+    add("pi", [], lambda q: g.iota(T.pi[:, :], [[0, 1]], 0, 1))
+    add("j4", [], lambda q: g.iota(T.j4[:, :], [[1, 4]], 0, 0, allow_small_or_imprecise_dtypes=True))
+    fill("one", T.one[:, :], 1.0)
+    fill("win0", T.win[:, 0:WO - 1], 0.0)
+    fill("win1", T.win[:, WO - 1:WO], -1e29)
+    ts("ai", ["pi"], T.ai[:, :], T.pi[:, :], 2, ALU.logical_shift_right, 3, ALU.bitwise_and)
+    ts("ii", ["pi"], T.ii[:, :], T.pi[:, :], 3, ALU.bitwise_and)
+    copy("af", ["ai"], T.af[:, :], T.ai[:, :])
+    copy("ic", ["ii"], T.ic[:, :], T.ii[:, :])
+    ts("ic4", ["ii"], T.ic4[:, :], T.ii[:, :], -4.0, ALU.add)
+    ts("w1", ["af", "j4"], T.w1[:, :], T.j4[:, :], T.af[:, 0:1], ALU.is_equal, UP, ALU.mult)
+    ts("w2", ["af", "j4"], T.w2[:, :], T.j4[:, :], T.af[:, 0:1], ALU.is_gt)
+    tt("w4", ["w1", "w2"], T.w4[:, :], T.w1[:, :], T.w2[:, :], ALU.add)
+    ts("w3", ["w4"], T.w4[:, 3:4], T.w4[:, 3:4], UP ** -2, ALU.mult)
+    for m in range(4):
+        add("wt%d" % m, ["one", "w3"], lambda q, m=m: A.activation(T.wt[:, m:W:4], T.one[:, 0:CM], ACT.Identity, scale=T.w4[:, m:m + 1]))
     hole = 4 * (NT + CN * r)
-    need("s", k_c)
-    did("s", A.activation(T.pa[:, hole:hole + 4 * CN], T.carry[:, 0:512], ACT.Copy, scale=0.0))
-    k_hole = did("s", A.activation(T.pb[:, hole:hole + 4 * CN], T.carry[:, 0:512], ACT.Copy, scale=0.0))
+    fill("holea", T.pa[:, hole:hole + 4 * CN], 0.0)
+    copy("holeb", ["holea"], T.pb[:, hole:hole + 4 * CN], T.pa[:, hole:hole + 4 * CN])
 
-    need("v", tok("d_ed"))
-    ts(T.pk1[0:16, :], T.eds[0:16, 0:32], 4.0, ALU.mult)
-    k = ts(T.pk2[0:16, :], T.eds[0:16, 32:64], 16384.0, ALU.mult)
-    need("v", tok("d_sn"))
-    k_of = {}
-    for t in (2, 3, 0, 1):
-        k_of[t] = ts(T["oft%d" % t][:, :], T.snl[:, :], 4.0, ALU.mult, float(XO + t), ALU.add)
-    need("v", k)
-    k = tt(T.pk[0:16, :], T.pk1[0:16, :], T.pk2[0:16, :], ALU.add)
-    need("v", k)
-    k_pkt = did("v", V.transpose(T.pkt[0:32, :], T.pk[0:32, :]))
-    need("y", k_pkt)
-    dma("y", "d_pr", T.prow[0:1, :], T.pkt[0:32, 0:16])
-    dma("y", "d_wb", T.wbb[:, :], T.wb[:, :])
-    dma("y", "d_nl", T.nld[:, :], T.nl[:, :])
-
-    need("v", tok("d_x"), k_xb)
-    need("s", tok("d_x"), k_xb)
+    spread("sn", "sn.0", T.snl)
+    for t in range(4):
+        ts("of%d" % t, ["sn2"], T["oft%d" % t][:, :], T.snl[:, :], 4.0, ALU.mult, float(t), ALU.add)
     for o, d in enumerate(others):
-        ks = []
-        for q, t in (("v", 0), ("v", 1), ("s", 2), ("s", 3)):
-            need(q, k_of[t])
-            ks.append(copy(q, T.ht[:, 512 * o + t:512 * o + 512:4], T.xb[:, :].indirect(T["oft%d" % t][:, 8 * d:8 * d + 8])))
-        need("v", *ks)
+        for t in range(4):
+            copy("n%d%d" % (o, t), ["x.0", "of%d" % t], T.ht[:, 512 * o + t:512 * o + 512:4], T.xb[:, :].indirect(T["oft%d" % t][:, 8 * d:8 * d + 8]))
         here, there = slice(CN * o, CN * o + CN), slice(CN * r, CN * r + CN)
-        k = did("v", V.quantize_mx(T.hq[:, here], T.hp[:, here], T.ht[:, 512 * o:512 * o + 512]))
-        need("g", k)
-        send(d, "lno", [(T.nnq[:, there].bitcast(dt.uint8), T.hq[:, here].bitcast(dt.uint8)), (T.nnp[:, there], T.hp[:, here])], "an%d" % r)
-    g.sem_inc(S.go, 1)
-    cnt["go"] = 1
-    need("y", tok("go"))
-    dma("y", "d_e", T.eb[:, XO:XO + 4 * E], T.e[:, :])
-    dma("y", "d_v", T.vb[:, :], T.v[:, :])
-    need("g", tok("d_pr"))
-    k_wn = did("g", g.partition_broadcast(T.wn[:, :], T.prow[0:1, :], 128))
-    need("g", tok("d_nl"), k_i4)
-    g.indirect_dma_start(T.nlr[:, :], None, T.nld[:, :], IndirectOffsetOnAxis(ap=T.i4i[:, 0:1], axis=0), bounds_check=3).then_inc(S.d_g, 16)
-    cnt["d_g"] = 16
+        quant("hq%d" % o, seq("n%d" % o, range(4)), T.hq[:, here], T.hp[:, here], T.ht[:, 512 * o:512 * o + 512])
+        send(("sn0", "sn1s", "sn2s")[o], ["hq%d" % o], d, "lno", "an%d" % r,
+             [(T.nnq[:, there].bitcast(dt.uint8), T.hq[:, here].bitcast(dt.uint8)), (T.nnp[:, there], T.hp[:, here])])
 
-    need("v", tok("d_wa"))
-    k_wq = did("v", V.quantize_mx(T.waq[:, :], T.wap[:, :], T.wab[:, :]))
-    k_xq = did("v", V.quantize_mx(T.xxq[:, :], T.xxp[:, :], T.xb[:, XO:XO + 1024]))
-    need("v", tok("d_wb"))
-    k_uq = did("v", V.quantize_mx(T.wbq[:, :], T.wbp[:, :], T.wbb[:, :]))
-
-    bank = [None] * 8
-    k_pw = []
-
-    def products(cq, cp, n, who):
-        ks = {}
-        for j in who:
-            c, p = (T.waq, T.wap) if j < 4 else (T.wbq, T.wbp)
+    quant("qa", ["wa.0"], T.waq[:, :], T.wap[:, :], T.wab[:, :])
+    quant("qb", ["wb.0"], T.wbq[:, :], T.wbp[:, :], T.wbb[:, :])
+    quant("qx", ["x.0"], T.xxq[:, :], T.xxp[:, :], T.xb[:, :])
+    quant("qv", ["v.0"], T.vvq[:, :], T.vvp[:, :], T.vb[:, :])
+    first = min(others[:2])
+    assert max(others[:2]) == first + 1
+    before = None
+    for name, deps, cq, cp, h, n in (("o", ["qx"], T.xxq[:, :], T.xxp[:, :], 0, NT),
+                                     ("f", seq("an", others[:2]), T.nnq[:, CN * first:CN * first + 2 * CN], T.nnp[:, CN * first:CN * first + 2 * CN], NT + CN * first, 2 * CN),
+                                     ("m", seq("an", others[2:]), T.nnq[:, CN * others[2]:CN * others[2] + CN], T.nnp[:, CN * others[2]:CN * others[2] + CN], NT + CN * others[2], CN)):
+        for j in range(8):
+            c, p, w, win = (T.waq, T.wap, "qa", T.pa) if j < 4 else (T.wbq, T.wbp, "qb", T.pb)
             b = slice(128 * (j % 4), 128 * (j % 4) + 128)
-            need("t", k_wq if j < 4 else k_uq)
-            if bank[j]:
-                need("t", bank[j])
-            ks[j] = did("t", PE.matmul_mx(T.ps[:, 512 * j:512 * j + n], c[:, b], p[:, b], cq, cp, True, True))
-        return ks
+            bank = T.ps[:, 512 * j:512 * j + n]
+            add("%sP%d" % (name, j), deps + [w] + (["%sC%d" % (before, j)] if before else []),
+                lambda q, bank=bank, c=c, p=p, b=b, cq=cq, cp=cp: PE.matmul_mx(bank, c[:, b], p[:, b], cq, cp, True, True))
+            copy("%sC%d" % (name, j), ["%sP%d" % (name, j)], win[:, 4 * h + j % 4:4 * h + 4 * n:4], bank)
+        before = name
+    pa_full = ["holea"] + [n + "C%d" % j for n in "ofm" for j in range(4)]
+    pb_full = ["holeb"] + [n + "C%d" % j for n in "ofm" for j in range(4, 8)]
 
-    def take(q, plan, h, n, ks):
-        for j in ks:
-            if plan[j] == q:
-                need(q, ks[j])
-                bank[j] = copy(q, (T.pa if j < 4 else T.pb)[:, 4 * h + j % 4:4 * h + 4 * n:4], T.ps[:, 512 * j:512 * j + n])
-                k_pw.append(bank[j])
+    ts("pk1", ["ed.0"], T.pk1[:, :], T.eds[:, 128:256], 8192.0, ALU.mult, 1.0, ALU.add)
+    tt("pk", ["pk1"], T.pk[:, :], T.eds[:, 0:128], T.pk1[:, :], ALU.add)
+    for k in range(4):
+        add("wn%d" % k, ["pk"], lambda q, k=k: g.partition_broadcast(T.wn[:, 128 * k:128 * k + 128], T.pk[32 * k:32 * k + 1, :], 128))
+    ts("k1", ["sm.0"], T.k1[0:32, :], T.sml[0:32, :], 4, ALU.arith_shift_right)
+    ts("k0", ["sm.0"], T.k0[0:32, :], T.sml[0:32, :], 15, ALU.bitwise_and)
+    ts("k2", ["k0"], T.k2[0:32, :], T.k0[0:32, :], 32.0, ALU.mult)
+    tt("k3", ["k1", "k2"], T.k3[0:32, :], T.k2[0:32, :], T.k1[0:32, :], ALU.add)
+    copy("smo", ["k3"], T.smo[0:32, :], T.k3[0:32, :])
+    spread("sm", "smo", T.smo)
+    copy("G", ["sm2"] + seq("wn", range(4)), T.gg[:, :], T.wn[:, :].indirect(T.smo[:, :]))
+    pick("scan", ["G"], T.sc, T.gg, W)
+    ts("ob", ["scan", "ic"], T.ob[:, :], T.sc[:, 3:W:4], UP / 2048, ALU.mult, T.ic[:, 0:1], ALU.add)
+    ts("ci", ["scan"], T.ci[:, :], T.sc[:, 3:W:4], UP, ALU.mult)
+    ts("cl", ["ci"], T.cl[:, :], T.ci[:, :], 2047, ALU.bitwise_and)
+    ts("oa", ["cl", "ic4"], T.oa[:, :], T.cl[:, :], 4.0, ALU.mult, T.ic4[:, 0:1], ALU.add)
+    add("smr.0", ["smd.0", "ai"] + seq("wn", range(4)), lambda q: g.indirect_dma_start(T.smr[:, :], None, T.smd[:, :], IndirectOffsetOnAxis(ap=T.ai[:, 0:1], axis=0), bounds_check=3))
+    for b in range(4):
+        ts("oe%d" % b, ["smr.0", "ic"], T.oe[:, b:144:4], T.smr[:, 36 * b:36 * b + 36], 4.0, ALU.mult, T.ic[:, 0:1], ALU.add)
 
-    need("t", k_xq)
-    own = (OWN, 0, NT, products(T.xxq[:, :], T.xxp[:, :], NT, range(8)))
-    take("s", *own)
-
-    need("v", tok("d_sm"))
-    k_smo = ts(T.smo[:, :], T.sml[:, :], 0.0, ALU.max)
-    need("v", k_smo, k_kk, k_mask)
-    k = tt(T.mv2[:, :], T.kk[:, :].indirect(T.smo[:, :]), T.mask[:, :], ALU.mult)
-    need("v", k, k_c)
-    k = did("v", V.tensor_tensor_scan(T.sc2[:, :], T.carry[:, :], T.mv2[:, :], 0.0, ALU.mult, ALU.add))
-    take("v", *own)
-    need("v", k, k_ic)
-    k_oe = ts(T.oe[:, :], T.sc2[:, 3:576:4], 4.0, ALU.mult, T.ic[:, 0:1], ALU.add)
-
-    def late(o):
-        s = others[o]
-        b = slice(CN * s, CN * s + CN)
-        need("t", ("an%d" % s, arrived(s)))
-        return LATE[o], NT + CN * s, CN, products(T.nnq[:, b], T.nnp[:, b], CN, (4, 5, 6, 7, 0, 1, 2, 3))
-
-    la = late(0)
-    take("s", *la)
-    need("v", k_wn)
-    k = tt(T.mv[:, :], T.wn[:, :].indirect(T.smo[:, :]), T.mask[:, :], ALU.mult)
-    need("v", k)
-    k = did("v", V.tensor_tensor_scan(T.sc[:, :], T.carry[:, :], T.mv[:, :], 0.0, ALU.mult, ALU.add))
-    take("v", *la)
-    need("v", k, k_ip)
-    k = ts(T.ci[:, :], T.sc[:, 3:576:4], T.ipk[:, 0:1], ALU.add)
-    lb = late(1)
-    take("s", *lb)
-    need("v", k)
-    kh = ts(T.co[:, 144:288], T.ci[:, :], 12, ALU.logical_shift_right)
-    kl = ts(T.co[:, 0:144], T.ci[:, :], 4095, ALU.bitwise_and)
-    take("v", *lb)
-    need("v", kh)
-    k_ob = copy("v", T.oab[:, 144:288], T.co[:, 144:288])
-    need("v", kl)
-    k_oa = copy("v", T.oab[:, 0:144], T.co[:, 0:144])
-    lc = late(2)
-    take("v", *lc)
-    take("s", *lc)
-
-    W, H = 4 * CM, 2 * CM
-    gb, uu, zz = ([T["%s%d" % (n, o)] for o in range(4)] for n in ("gb", "uu", "zz"))
-    k_gb, k_u, k_z, k_r, k_q = {}, {}, {}, {}, {}
-
-    def list_of(t, base, o, a=0, n=36):
-        c = base + 36 * blocks[o] + a
-        return t[:, c:c + n]
-
-    def gather_b(q, o, a=0, b=W):
-        need(q, *k_pw, k_hole, k_ob)
-        k_gb.setdefault(o, []).append(copy(q, gb[o][:, a:b], T.pb[:, :].indirect(list_of(T.oab, 144, o, a // 16, (b - a) // 16))))
-
-    def add_a(o):
-        need("v", *k_pw, k_hole, k_oa, *k_gb[o])
-        k_u[o] = tt(uu[o][:, :], T.pa[:, :].indirect(list_of(T.oab, 0, o)), gb[o][:, :], ALU.add)
-
-    def add_e(o):
-        need("v", tok("d_e"), k_eb, k_oe, k_u[o])
-        k_z[o] = tt(zz[o][:, :], T.eb[:, :].indirect(list_of(T.oe, 0, o)), uu[o][:, :], ALU.add)
-
-    def relu(q, o, a, b):
-        need(q, k_z[o])
-        out = T.mt[:, W * o + a:W * o + b]
-        if q == "s":
-            k = did("s", A.activation(out, zz[o][:, a:b], ACT.Relu, scale=0.05))
-        else:
-            k = ts(out, zz[o][:, a:b], 0.0, ALU.max, 0.05, ALU.mult)
-        k_r.setdefault(o, []).append(k)
-
-    def quant(o):
-        need("v", *k_r[o])
+    for o, d in enumerate(blocks):
+        gb, uu, zz = (T["%s%d" % (n, o)] for n in ("gb", "uu", "zz"))
+        c = 36 * d
+        halves = (("a", 0, H), ("b", H, W))
+        for x, a, b in (("", 0, W),) + halves:
+            copy("B%d%s" % (o, x), pb_full + ["ob"], gb[:, a:b], T.pb[:, :].indirect(T.ob[:, c + a // 16:c + b // 16]))
+            add("R%d%s" % (o, x), ["E%d" % o], lambda q, out=T.mt[:, W * o + a:W * o + b], in_=zz[:, a:b]:
+                A.activation(out, in_, ACT.Relu, scale=0.05) if q == "s" else V.tensor_scalar(out, in_, 0.0, 0.05, ALU.max, ALU.mult))
+        tt("A%d" % o, pa_full + ["oa", "B%d" % o], uu[:, :], T.pa[:, :].indirect(T.oa[:, c:c + 36]), gb[:, :], ALU.add)
+        tt("E%d" % o, ["e.0", "A%d" % o] + seq("oe", range(4)), zz[:, :], T.eb[:, :].indirect(T.oe[:, c:c + 36]), uu[:, :], ALU.add)
         here, there = slice(CM * o, CM * o + CM), slice(CM * r, CM * r + CM)
-        k_q[o] = did("v", V.quantize_mx(T.mmq[:, here], T.mmp[:, here], T.mt[:, W * o:W * o + W]))
-        if blocks[o] != r:
-            need("g", k_q[o])
-            send(blocks[o], "lme", [(T.rrq[:, there].bitcast(dt.uint8), T.mmq[:, here].bitcast(dt.uint8)), (T.rrp[:, there], T.mmp[:, here])], "am%d" % r)
+        quant("Q%d" % o, ["R%d" % o], T.mmq[:, here], T.mmp[:, here], T.mt[:, W * o:W * o + W])
+        if d != r:
+            send("sm%ds" % o, ["Q%d" % o], d, "lme", "am%d" % r,
+                 [(T.rrq[:, there].bitcast(dt.uint8), T.mmq[:, here].bitcast(dt.uint8)), (T.rrp[:, there], T.mmp[:, here])])
 
-    gather_b("s", 0, 0, H)
-    gather_b("v", 0, H, W)
-    gather_b("s", 1)
-    gather_b("s", 2)
-    add_a(0)
-    add_e(0)
-    relu("s", 0, 0, W)
-    add_a(1)
-    gather_b("s", 3)
-    add_e(1)
-    quant(0)
-    relu("s", 1, 0, W)
-    add_a(2)
-    quant(1)
-    add_e(2)
-    relu("s", 2, 0, H)
-    relu("v", 2, H, W)
-    quant(2)
-    add_a(3)
-    need("v", tok("d_g"))
-    k = tt(T.nmv[:, :], T.nlr[:, :], T.mask[:, 0:256], ALU.mult)
-    need("v", tok("d_v"))
-    k_vq = did("v", V.quantize_mx(T.vvq[:, :], T.vvp[:, :], T.vb[:, :]))
-    add_e(3)
-    need("v", k)
-    k = did("v", V.tensor_tensor_scan(T.nsc[:, :], T.carry[:, 0:256], T.nmv[:, :], 0.0, ALU.mult, ALU.add))
-    relu("s", 3, 0, H)
-    relu("v", 3, H, W)
-    need("v", k)
-    k = tt(T.nt1[:, :], T.nsc[:, 3:128:4], T.nsc[:, 131:256:4], ALU.max)
-    quant(3)
-    need("v", k)
-    k = tt(T.nt2[:, :], T.nt1[:, 0:16], T.nt1[:, 16:32], ALU.max)
-    ts(T.onl[:, 16:64], T.nsc[:, 67:256:4], float(WO), ALU.add)
-    need("v", k)
-    k = ts(T.nt3[:, :], T.nt2[:, :], 0.0, ALU.is_lt)
-    need("v", k)
-    k = tt(T.nt4[:, :], T.nsc[:, 3:64:4], T.nt3[:, :], ALU.subtract)
-    need("v", k)
-    k_onl = ts(T.onl[:, 0:16], T.nt4[:, :], float(WO), ALU.add)
+    add("nlr.0", ["nld.0", "ii"], lambda q: g.indirect_dma_start(T.nlr[:, :], None, T.nld[:, :], IndirectOffsetOnAxis(ap=T.ii[:, 0:1], axis=0), bounds_check=3))
+    ts("nl1", ["nlr.0"], T.nmv[:, :], T.nlr[:, :], 2.0, ALU.add)
+    pick("nl2", ["nl1"], T.nsc, T.nmv, NT)
+    tt("nl3", ["nl2"], T.nt1[:, :], T.nsc[:, 3:128:4], T.nsc[:, 131:256:4], ALU.max)
+    tt("nl4", ["nl3"], T.nt2[:, :], T.nt1[:, 0:16], T.nt1[:, 16:32], ALU.max)
+    ts("nl5", ["nl2"], T.onl[:, 16:64], T.nsc[:, 67:256:4], UP, ALU.mult, WO - 2.0, ALU.add)
+    ts("nl6", ["nl4"], T.nt3[:, :], T.nt2[:, :], 1.5 / UP, ALU.is_lt, 1.0 / UP, ALU.mult)
+    tt("nl7", ["nl6"], T.nt4[:, :], T.nsc[:, 3:64:4], T.nt3[:, :], ALU.subtract)
+    ts("nl8", ["nl7"], T.onl[:, 0:16], T.nt4[:, :], UP, ALU.mult, WO - 2.0, ALU.add)
 
-    need("t", k_vq)
-    k_w = []
-    for n, o in enumerate((0, 3, 1, 2)):
+    for n, o in enumerate((0, 1, 3, 2)):
         s = blocks[o]
         if s == r:
-            need("t", k_q[o])
-            cq, cp = T.mmq[:, CM * o:CM * o + CM], T.mmp[:, CM * o:CM * o + CM]
+            dep, cq, cp = "Q%d" % o, T.mmq[:, CM * o:CM * o + CM], T.mmp[:, CM * o:CM * o + CM]
         else:
-            need("t", ("am%d" % s, arrived(s)))
-            cq, cp = T.rrq[:, CM * s:CM * s + CM], T.rrp[:, CM * s:CM * s + CM]
-        need("t", bank[n])
-        k = did("t", PE.matmul_mx(T.ps[:, 512 * n:512 * n + CM], T.vvq[:, :], T.vvp[:, :], cq, cp, True, True))
-        need("s", k)
-        k_w.append(copy("s", T.win[:, WO + CM * s:WO + CM * s + CM], T.ps[:, 512 * n:512 * n + CM]))
+            dep, cq, cp = "am%d" % s, T.rrq[:, CM * s:CM * s + CM], T.rrp[:, CM * s:CM * s + CM]
+        bank = T.ps[:, 512 * n:512 * n + CM]
+        add("vP%d" % n, ["qv", dep, "mC%d" % n], lambda q, bank=bank, cq=cq, cp=cp: PE.matmul_mx(bank, T.vvq[:, :], T.vvp[:, :], cq, cp, True, True))
+        copy("vC%d" % n, ["vP%d" % n], T.win[:, WO + CM * s:WO + CM * s + CM], bank)
 
-    def at(f, a, b):
-        return T.win[:, :].indirect(T.onl[:, 16 * f + a // 16:16 * f + b // 16])
+    ready = ["win0", "win1", "nl5", "nl8"] + seq("vC", range(4))
+    for k, (x, a, b) in enumerate((("a", 0, NA), ("b", NA, NT))):
+        steps = (T.g0, T.m1, T.m2, T.yb)
+        for f in range(4):
+            at = T.win[:, :].indirect(T.onl[:, 16 * f + a // 16:16 * f + b // 16])
+            if f == 0:
+                copy("y0" + x, ready, T.g0[:, a:b], at)
+            else:
+                tt("y%d%s" % (f, x), ready + ["y%d%s" % (f - 1, x)], steps[f][:, a:b], at, steps[f - 1][:, a:b], ALU.max)
+        dma("y.%d" % k, ["y3" + x], T.y[:, a:b], T.yb[:, a:b])
 
-    def largest(f, a, b, k):
-        i, o = (None, (T.g0, T.m1), (T.m1, T.m2), (T.m2, T.yb))[f]
-        need("v", k)
-        return tt(o[:, a:b], at(f, a, b), i[:, a:b], ALU.max)
+    silent = ["go"] + [n for n in ORDER["g"] if n == "sn0" or n.endswith("s")]
+    total = {"go": 1}
+    total.update(sent)
+    for q in ORDER:
+        for n in ORDER[q]:
+            if n not in silent:
+                k, step = ("d_" + n.split(".")[0], 16) if "." in n else ("c" + q, 1)
+                total[k] = total.get(k, 0) + step
+                tok[n] = (k, total[k])
+    for n in list(tok):
+        if "." in n:
+            tok[n] = (tok[n][0], total[tok[n][0]])
+    seen = {}
 
-    need("s", k_onl, k_win, *k_w)
-    need("v", k_onl, k_win, *k_w)
-    kb = copy("s", T.g0[:, NA:NT], at(0, NA, NT))
-    ka = copy("v", T.g0[:, 0:NA], at(0, 0, NA))
-    ka = largest(1, 0, NA, ka)
-    ka = largest(2, 0, NA, ka)
-    kb = largest(1, NA, NT, kb)
-    ka = largest(3, 0, NA, ka)
-    kb = largest(2, NA, NT, kb)
-    kb = largest(3, NA, NT, kb)
-    need("y", ka)
-    dma("y", "d_y", T.y[:, 0:NA], T.yb[:, 0:NA])
-    need("y", kb)
-    dma("y", "d_y", T.y[:, NA:NT], T.yb[:, NA:NT])
+    def need(q, toks):
+        best = {}
+        for k, c in toks:
+            best[k] = max(best.get(k, 0), c)
+        for k in best:
+            if seen.get((q, k), 0) < best[k]:
+                Q[q].wait_ge(S[k], best[k])
+                seen[(q, k)] = best[k]
 
-    for k in cnt:
-        need("g", tok(k))
-    for s in others:
-        need("g", ("an%d" % s, arrived(s)), ("am%d" % s, arrived(s)))
+    for q in ORDER:
+        for n in ORDER[q]:
+            deps, fn = task[n]
+            need(q, [tok[x] for d in deps for x in ([d] if d in tok else [d + "a", d + "b"])])
+            ins = fn(q)
+            if n not in silent:
+                ins.then_inc(S[tok[n][0]], 16 if "." in n else 1)
+    need("g", list(total.items()) + [tok[n] for n in seq("an", others) + seq("am", others)])

@@ -7,6 +7,8 @@ WO = 8
 NA = 64
 W, H = 4 * CM, 2 * CM
 UP = 2.0 ** 24
+PARTS = ((None, None), (None, None), (None, None))
+PIECES = {"": (0, W), "a": (0, H), "b": (H, W), "c": (H, H + CM), "d": (H + CM, W)}
 ALU, ACT = AluOpType, ActivationFunctionType
 
 SCRATCH = {
@@ -19,18 +21,17 @@ SCRATCH = {
     "mt": ("sbuf", [128, 4 * N * CM], "bfloat16"),
     "pa": ("sbuf", [128, 4 * NH], "float32"),
     "pb": ("sbuf", [128, 4 * NH], "float32"),
-    "nld": ("dram", [4, 256], "int32"),
     "smd": ("dram", [4, 144], "int32"),
     "ps": ("psum", [128, 4096], "float32"),
 }
-for _n, _w in (("snl", 32), ("sml", 36), ("eds", 256), ("nlr", 256), ("smr", 144), ("pi", 1), ("ai", 1), ("ii", 1), ("ci", 144), ("cl", 144),
-               ("k0", 36), ("k1", 36), ("k2", 36), ("k3", 36)):
+for _n, _w in (("snl", 32), ("sml", 36), ("eds", 64), ("nlr", 256), ("smr", 144), ("pi", 1), ("ai", 1), ("ii", 1), ("ci", 144), ("cl", 144),
+               ("rpi", 32)):
     SCRATCH[_n] = ("sbuf", [128, _w], "int32")
-for _n, _w in (("pk1", 128), ("pk", 128), ("wn", 512), ("af", 1), ("ic", 1), ("ic4", 1), ("j4", 4), ("w1", 4), ("w2", 4),
+for _n, _w in (("pk0", 16), ("pk", 16), ("wide", E), ("tr", 128), ("trt", 128), ("wn", E), ("af", 1), ("ic", 1), ("ic4", 1), ("j4", 4), ("w1", 4), ("w2", 4),
                ("w4", 4), ("one", CM), ("wt", W), ("gg", W), ("sc", W), ("nmv", 256), ("nsc", 256), ("nt1", 32), ("nt2", 16), ("nt3", 16),
                ("nt4", 16), ("win", WO + N * CM), ("g0", NT), ("m1", NT), ("m2", NT), ("yb", NT)):
     SCRATCH[_n] = ("sbuf", [128, _w], "float32")
-for _n, _w in (("smo", 36), ("oe", 144), ("oa", 144), ("ob", 144), ("onl", 64), ("oft0", 32), ("oft1", 32), ("oft2", 32), ("oft3", 32)):
+for _n, _w in (("rp", 32), ("smo", 36), ("oe", 144), ("oa", 144), ("ob", 144), ("onl", 64), ("oft0", 32), ("oft1", 32), ("oft2", 32), ("oft3", 32)):
     SCRATCH[_n] = ("sbuf", [128, _w], "uint16")
 for _k in range(4):
     for _n in ("gb", "uu", "zz"):
@@ -39,7 +40,7 @@ for _n, _w in (("h", 3 * CN), ("nn", N * CN), ("xx", NT), ("wa", 512), ("wb", 51
     SCRATCH[_n + "q"] = ("sbuf", [128, _w], "float8_e4m3fn_x4")
     SCRATCH[_n + "p"] = ("sbuf", [128, _w], "uint8")
 
-LOADS = ["sn", "x", "ed", "wa", "wb", "sm", "smd", "nld", "e", "v", "smr", "nlr", "y"]
+LOADS = ["sn", "x", "ed", "wa", "wb", "wl", "sm", "smd", "sg", "nl", "e", "v", "smr", "y", "ac0", "ac1", "ac2", "ac3"]
 SEMAPHORES = ["cv", "cs", "ct", "cg", "lno", "lme", "go"] + ["d_" + _n for _n in LOADS] + ["an%d" % _k for _k in range(4)] + ["am%d" % _k for _k in range(4)]
 
 
@@ -48,17 +49,19 @@ def seq(name, items):
 
 
 ORDER = {
-    "y": "sn.0 x.0 ed.0 sm.0 smd.0 smd.1 nld.0 wb.0 e.0 v.0 y.0 y.1",
-    "s": "sn.1 x.1 ed.1 sm.1 smd.2 smd.3 wa.0 wt0 wt1 wt2 wt3 "
-         "n02 n03 n12 n13 n11 n22 n23 n21 holeb oC0 oC1 oC2 oC3 G oC6 fC4 fC1 fC0 fC6 fC2 mC4 mC6 mC1 mC0 mC2 B0a "
-         "B1 B2 R0 B3 R1 R2a R3a R3b vC0 vC1 vC3 vC2 y0b",
-    "v": "ed0 ai one af ii w1 w2 ic w4 ic4 w3 sn1 win0 sn2 win1 of2 of3 of0 of1 "
-         "n00 n01 pk1 hq0 n10 pk hq1 n20 k0 k1 qx k2 hq2 k3 qa smo sm1 sm2 qb "
-         "oC4 oC5 oC7 scan fC5 ci ob cl fC7 oa fC3 mC5 mC7 mC3 B0b oe0 oe1 oe2 oe3 "
-         "A0 A1 E0 A2 E1 Q0 E2 Q1 nl1 R2b qv Q2 A3 nl2 E3 nl3 nl5 nl4 nl6 nl7 Q3 nl8 "
+    "y": "sn.0 x.0 ed.0 ed.1 wb.0 sm.0 sm.1 sm.2 sm.3 sm.4 sm.5 sm.6 sm.7 smd.0 smd.1 smd.2 smd.3 nl.0 nl.1 nl.2 nl.3 nl.4 nl.5 nl.6 nl.7 e.0 v.0 y.0 y.1",
+    "s": "sn.1 x.1 ed.2 ed.3 wa.0 wt0 wt1 wt2 "
+         "n02 n03 n12 n13 n21 pk1 n22 pk2 n23 wide oC0 oC1 oC2 oC3 G oC4 oC6 "
+         "fC4 fC5 fC6 fC7 fC0 fC1 fC2 fC3 pC4 pC6 pC0 pC2 mC4 mC6 B0a mC1 mC3 "
+         "B1 B2 R0 R1 B3 R2a R2b R3a R3c vC0 vC1 vC3 y0b",
+    "v": "one win0 ai win1 af rp w1 w2 sn1 w4 sn2 ii of2 of3 of0 of1 "
+         "n00 n01 pk0 hq0 pk n10 n11 qx hq1 qa n20 smo hq2 wn qb nl1 wt3 ic oC5 nl2 oC7 nl3 scan nl4 "
+         "ci ob cl nl6 oa pC5 pC7 pC1 pC3 oe0 oe1 oe2 oe3 mC5 mC7 B0b mC0 mC2 nl7 "
+         "A0 A1 E0 E1 Q0 A2 Q1 E2a E2b A3a Q2 A3b qv E3a E3b nl8 R3d nl9 Q3 on vC2 "
          "y0a y1a y1b y2a y2b y3a y3b",
-    "t": "oP0 oP1 oP2 oP3 oP4 oP5 oP7 oP6 fP4 fP5 fP1 fP0 fP7 fP6 fP3 fP2 mP5 mP4 mP7 mP6 mP1 mP0 mP3 mP2 vP0 vP1 vP3 vP2",
-    "g": "pi j4 holea sn0 wn0 sn1s sn2s go wn1 wn2 wn3 smr.0 nlr.0 sm0s sm1s sm2s",
+    "t": "oP0 oP1 oP2 oP3 oP4 oP5 oP6 oP7 fP4 fP5 fP6 fP7 fP0 fP1 fP2 fP3 pP4 pP5 pP6 pP7 pP0 pP1 pP2 pP3 "
+         "mP4 mP5 mP6 mP7 mP0 mP1 mP2 mP3 vP0 vP1 vP3 vP2",
+    "g": "pi j4 rp0 holea sn0 sn1s sn2s smr.0 go holeb sm0s sm1s sm2s",
 }
 ORDER = {_q: ORDER[_q].split() for _q in ORDER}
 
@@ -70,6 +73,8 @@ def rank_program(g, core, T, topo):
     S = T.sem
     Q = {"g": g, "v": g.vector, "s": g.scalar, "t": g.tensor, "y": g.sync}
     V, A, PE = g.vector, g.scalar, g.tensor
+    EARLY = 4 if "ql" not in ORDER["v"] else 3 if ORDER["t"].index("oP2") < 8 else 2
+    listed = [n for q in ORDER for n in ORDER[q]]
     task = {}
     tok = {}
 
@@ -78,9 +83,6 @@ def rank_program(g, core, T, topo):
         return 2 if topo.mates(a, b) else 1 if topo.same_plane(a, b) else 0
     others = sorted([d for d in range(N) if d != r], key=near)
     blocks = others + [r]
-    for s in others:
-        n = 2 * len(topo.engines(T.cores[s], core))
-        tok["an%d" % s], tok["am%d" % s] = ("an%d" % s, n), ("am%d" % s, n)
 
     def add(name, deps, fn):
         task[name] = (deps, fn)
@@ -106,38 +108,51 @@ def rank_program(g, core, T, topo):
     def quant(name, deps, c, p, in_):
         add(name, deps, lambda q: V.quantize_mx(c, p, in_))
 
-    def pick(name, deps, out, in_, n):
-        add(name, deps + seq("wt", range(4)), lambda q: V.tensor_tensor_scan(out[:, :], in_[:, :], T.wt[:, 0:n], 0.0, ALU.max, ALU.mult))
+    def pick(name, deps, out, in_, n, p=128):
+        add(name, deps + seq("wt", range(4)), lambda q: V.tensor_tensor_scan(out[0:p, :], in_[0:p, :], T.wt[0:p, 0:n], 0.0, ALU.max, ALU.mult))
 
     sent = {"lno": 0, "lme": 0}
 
-    def send(name, deps, d, lsem, rsem, pairs):
+    def engines(src, dst, part):
+        e = topo.engines(src, dst)
+        return e if part is None else e[part * len(e) // 2:(part + 1) * len(e) // 2]
+
+    def send(name, deps, d, lsem, rsem, pairs, parts=(None, None)):
         dst = T.cores[d]
         rid, pid, _ = topo.addr(dst)
-        sent[lsem] += len(pairs) * len(topo.engines(core, dst))
+        sent[lsem] += sum(len(engines(core, dst, p)) for p in parts)
 
         def fn(q):
-            for o, i in pairs:
-                g.remote_dma(o, i, S[rsem], S[lsem], pid, rid, topo.mask(core, dst))
+            for (o, i), p in zip(pairs, parts):
+                g.remote_dma(o, i, S[rsem], S[lsem], pid, rid, sum(1 << e for e in engines(core, dst, p)))
         add(name, deps, fn)
+
+    for o, s in enumerate(others):
+        tok["an%d" % s] = ("an%d" % s, sum(len(engines(T.cores[s], core, p)) for p in PARTS[o]))
+        tok["am%d" % s] = ("am%d" % s, 2 * len(topo.engines(T.cores[s], core)))
 
     def spread(name, dep, t):
         copy(name + "1", [dep], t[32:64, :], t[0:32, :])
         copy(name + "2", [name + "1"], t[64:128, :], t[0:64, :])
 
-    for k in range(2):
+    for k in range(8):
         dma("sn.%d" % k, [], T.snl[16 * k:16 * k + 16, :], T.sn[:, :])
-        dma("sm.%d" % k, [], T.sml[16 * k:16 * k + 16, :], T.sm[:, :])
+    for k in range(2):
         dma("x.%d" % k, [], T.xb[64 * k:64 * k + 64, :], T.x[64 * k:64 * k + 64, :])
-    fill("ed0", T.eds[:, :], 0)
-    dma("ed.0", ["ed0"], T.eds[0:128:32, 0:128], T.es[:, :])
-    dma("ed.1", ["ed0"], T.eds[0:128:32, 128:256], T.ed[:, :])
-    dma("wa.0", [], T.wab[:, :], T.wa[:, :])
+    for k in range(8):
+        dma("sm.%d" % k, [], T.sml[16 * k:16 * k + 16, :], T.sm[:, :])
+    for h in range(2):
+        dma("ed.%d" % h, [], T.eds[16 * h:16 * h + 16, 0:31], T.es[:, h:h + 31])
+        dma("ed.%d" % (h + 2), [], T.eds[16 * h:16 * h + 16, 32:63], T.ed[:, h:h + 31])
+    dma("wa.0", [], T.wab[:, 0:512 * EARLY], T.wa[:, 0:512 * EARLY])
+    if EARLY < 4:
+        dma("wl.0", ["go"], T.wab[:, 512 * EARLY:2048], T.wa[:, 512 * EARLY:2048])
+        quant("ql", ["wl.0"], T.waq[:, 128 * EARLY:512], T.wap[:, 128 * EARLY:512], T.wab[:, 512 * EARLY:2048])
     dma("wb.0", [], T.wbb[:, :], T.wb[:, :])
     for a in range(4):
         dma("smd.%d" % a, [], T.smd[a:a + 1, :], T.sm[a:16:4, :])
-    dma("nld.0", [], T.nld[:, :], T.nl[:, :])
-    dma("e.0", ["go"], T.eb[:, :], T.e[:, :])
+        dma("sg.%d" % a, [], T.smd[a:a + 1, :], T.sm[a:16:4, :])
+    dma("e.0", ["go"] if "go" in ORDER["g"] else [], T.eb[:, :], T.e[:, :])
     dma("v.0", [], T.vb[:, :], T.v[:, :])
     add("go", [], lambda q: g.sem_inc(S.go, 1))
     tok["go"] = ("go", 1)
@@ -151,94 +166,121 @@ def rank_program(g, core, T, topo):
     ts("ii", ["pi"], T.ii[:, :], T.pi[:, :], 3, ALU.bitwise_and)
     copy("af", ["ai"], T.af[:, :], T.ai[:, :])
     copy("ic", ["ii"], T.ic[:, :], T.ii[:, :])
-    ts("ic4", ["ii"], T.ic4[:, :], T.ii[:, :], -4.0, ALU.add)
     ts("w1", ["af", "j4"], T.w1[:, :], T.j4[:, :], T.af[:, 0:1], ALU.is_equal, UP, ALU.mult)
     ts("w2", ["af", "j4"], T.w2[:, :], T.j4[:, :], T.af[:, 0:1], ALU.is_gt)
     tt("w4", ["w1", "w2"], T.w4[:, :], T.w1[:, :], T.w2[:, :], ALU.add)
-    ts("w3", ["w4"], T.w4[:, 3:4], T.w4[:, 3:4], UP ** -2, ALU.mult)
-    for m in range(4):
-        add("wt%d" % m, ["one", "w3"], lambda q, m=m: A.activation(T.wt[:, m:W:4], T.one[:, 0:CM], ACT.Identity, scale=T.w4[:, m:m + 1]))
+    for m in range(3):
+        add("wt%d" % m, ["one", "w4"], lambda q, m=m: A.activation(T.wt[:, m:W:4], T.one[:, :], ACT.Identity, scale=T.w4[:, m:m + 1]))
+    ts("wt3", ["one", "w4"], T.wt[:, 3:W:4], T.one[:, :], T.w4[:, 3:4], ALU.mult, UP ** -2, ALU.mult)
     hole = 4 * (NT + CN * r)
     fill("holea", T.pa[:, hole:hole + 4 * CN], 0.0)
-    copy("holeb", ["holea"], T.pb[:, hole:hole + 4 * CN], T.pa[:, hole:hole + 4 * CN])
+    if "holeb" not in ORDER["s"]:
+        fill("holeb", T.pb[:, hole:hole + 4 * CN], 0.0)
+    else:
+        copy("holeb", ["holea"], T.pb[:, hole:hole + 4 * CN], T.pa[:, hole:hole + 4 * CN])
 
     spread("sn", "sn.0", T.snl)
     for t in range(4):
-        ts("of%d" % t, ["sn2"], T["oft%d" % t][:, :], T.snl[:, :], 4.0, ALU.mult, float(t), ALU.add)
+        ts("of%d" % t, ["sn2" if "sn2" in listed else "sn.0"], T["oft%d" % t][:, :], T.snl[:, :], 4.0, ALU.mult, float(t), ALU.add)
     for o, d in enumerate(others):
         for t in range(4):
             copy("n%d%d" % (o, t), ["x.0", "of%d" % t], T.ht[:, 512 * o + t:512 * o + 512:4], T.xb[:, :].indirect(T["oft%d" % t][:, 8 * d:8 * d + 8]))
         here, there = slice(CN * o, CN * o + CN), slice(CN * r, CN * r + CN)
         quant("hq%d" % o, seq("n%d" % o, range(4)), T.hq[:, here], T.hp[:, here], T.ht[:, 512 * o:512 * o + 512])
         send(("sn0", "sn1s", "sn2s")[o], ["hq%d" % o], d, "lno", "an%d" % r,
-             [(T.nnq[:, there].bitcast(dt.uint8), T.hq[:, here].bitcast(dt.uint8)), (T.nnp[:, there], T.hp[:, here])])
+             [(T.nnq[:, there].bitcast(dt.uint8), T.hq[:, here].bitcast(dt.uint8)), (T.nnp[:, there], T.hp[:, here])], PARTS[o])
 
-    quant("qa", ["wa.0"], T.waq[:, :], T.wap[:, :], T.wab[:, :])
+    quant("qa", ["wa.0"], T.waq[:, 0:128 * EARLY], T.wap[:, 0:128 * EARLY], T.wab[:, 0:512 * EARLY])
     quant("qb", ["wb.0"], T.wbq[:, :], T.wbp[:, :], T.wbb[:, :])
     quant("qx", ["x.0"], T.xxq[:, :], T.xxp[:, :], T.xb[:, :])
     quant("qv", ["v.0"], T.vvq[:, :], T.vvp[:, :], T.vb[:, :])
-    first = min(others[:2])
-    assert max(others[:2]) == first + 1
-    before = None
-    for name, deps, cq, cp, h, n in (("o", ["qx"], T.xxq[:, :], T.xxp[:, :], 0, NT),
-                                     ("f", seq("an", others[:2]), T.nnq[:, CN * first:CN * first + 2 * CN], T.nnp[:, CN * first:CN * first + 2 * CN], NT + CN * first, 2 * CN),
-                                     ("m", seq("an", others[2:]), T.nnq[:, CN * others[2]:CN * others[2] + CN], T.nnp[:, CN * others[2]:CN * others[2] + CN], NT + CN * others[2], CN)):
-        for j in range(8):
-            c, p, w, win = (T.waq, T.wap, "qa", T.pa) if j < 4 else (T.wbq, T.wbp, "qb", T.pb)
-            b = slice(128 * (j % 4), 128 * (j % 4) + 128)
-            bank = T.ps[:, 512 * j:512 * j + n]
-            add("%sP%d" % (name, j), deps + [w] + (["%sC%d" % (before, j)] if before else []),
-                lambda q, bank=bank, c=c, p=p, b=b, cq=cq, cp=cp: PE.matmul_mx(bank, c[:, b], p[:, b], cq, cp, True, True))
-            copy("%sC%d" % (name, j), ["%sP%d" % (name, j)], win[:, 4 * h + j % 4:4 * h + 4 * n:4], bank)
-        before = name
-    pa_full = ["holea"] + [n + "C%d" % j for n in "ofm" for j in range(4)]
-    pb_full = ["holeb"] + [n + "C%d" % j for n in "ofm" for j in range(4, 8)]
+    def product(name, deps, wq, wp, cq, cp, n, out):
+        k = ORDER["t"].index(name)
+        bank = T.ps[:, 512 * (k % 8):512 * (k % 8) + n]
+        add(name, deps + [x.replace("P", "C") for x in ORDER["t"][max(k - 8, 0):max(k - 7, 0)]], lambda q: PE.matmul_mx(bank, wq, wp, cq, cp, True, True))
+        copy(name.replace("P", "C"), [name], out, bank)
 
-    ts("pk1", ["ed.0"], T.pk1[:, :], T.eds[:, 128:256], 8192.0, ALU.mult, 1.0, ALU.add)
-    tt("pk", ["pk1"], T.pk[:, :], T.eds[:, 0:128], T.pk1[:, :], ALU.add)
-    for k in range(4):
-        add("wn%d" % k, ["pk"], lambda q, k=k: g.partition_broadcast(T.wn[:, 128 * k:128 * k + 128], T.pk[32 * k:32 * k + 1, :], 128))
-    ts("k1", ["sm.0"], T.k1[0:32, :], T.sml[0:32, :], 4, ALU.arith_shift_right)
-    ts("k0", ["sm.0"], T.k0[0:32, :], T.sml[0:32, :], 15, ALU.bitwise_and)
-    ts("k2", ["k0"], T.k2[0:32, :], T.k0[0:32, :], 32.0, ALU.mult)
-    tt("k3", ["k1", "k2"], T.k3[0:32, :], T.k2[0:32, :], T.k1[0:32, :], ALU.add)
-    copy("smo", ["k3"], T.smo[0:32, :], T.k3[0:32, :])
-    spread("sm", "smo", T.smo)
-    copy("G", ["sm2"] + seq("wn", range(4)), T.gg[:, :], T.wn[:, :].indirect(T.smo[:, :]))
+    groups = {"f": others[:1], "p": others[1:2], "d": others[:2], "m": others[2:]}
+    assert max(groups["d"]) == min(groups["d"]) + 1
+    pa_full, pb_full = ["holea"], ["holeb"]
+    for name in ORDER["t"]:
+        j = int(name[2])
+        if name[0] == "o":
+            deps, cq, cp, h, n = ["qx"], T.xxq[:, :], T.xxp[:, :], 0, NT
+        elif name[0] in groups:
+            c, n = CN * min(groups[name[0]]), CN * len(groups[name[0]])
+            deps, cq, cp, h = seq("an", groups[name[0]]), T.nnq[:, c:c + n], T.nnp[:, c:c + n], NT + c
+        else:
+            continue
+        c, p, w, win, full = (T.waq, T.wap, "qa" if j < EARLY else "ql", T.pa, pa_full) if j < 4 else (T.wbq, T.wbp, "qb", T.pb, pb_full)
+        b = slice(128 * (j % 4), 128 * (j % 4) + 128)
+        product(name, deps + [w], c[:, b], p[:, b], cq, cp, n, win[:, 4 * h + j % 4:4 * h + 4 * n:4])
+        full.append(name.replace("P", "C"))
+
+    ts("pk0", ["ed.0"], T.pk0[0:32, :], T.eds[0:32, 32:63:2], 8192.0, ALU.mult, 1.0, ALU.add)
+    tt("pk", ["pk0"], T.pk[0:32, :], T.eds[0:32, 0:31:2], T.pk0[0:32, :], ALU.add)
+    spread("pk", "pk", T.pk)
+    add("rp0", [], lambda q: g.iota(T.rpi[:, :], [[1, 16], [0, 2]], 0, 0))
+    copy("rp", ["rp0"], T.rp[:, :], T.rpi[:, :])
+    copy("wide", ["pk2", "rp"], T.wide[:, :], T.pk[:, :].indirect(T.rp[:, :]))
+    add("wn", ["wide"], lambda q: V.transpose(T.wn[:, :], T.wide[:, :]))
+    copy("smo", ["sm.0"], T.smo[:, :], T.sml[:, :])
+    fill("tz", T.tr[:, :], 0.0)
+    for a in range(4):
+        tt("pq%d" % a, ["pk0", "tz"], T.tr[32 * a:32 * a + 32, 0:128:32], T.eds[0:32, 8 * a:8 * a + 7:2], T.pk0[0:32, 4 * a:4 * a + 4], ALU.add)
+        add("wn%d" % a, ["trp"], lambda q, a=a: g.partition_broadcast(T.wn[:, 128 * a:128 * a + 128], T.trt[32 * a:32 * a + 1, :], 128))
+    add("trp", seq("pq", range(4)), lambda q: V.transpose(T.trt[:, :], T.tr[:, :]))
+    spread_by = ["wn"] if "wn" in listed else seq("wn", range(4))
+    copy("G", ["smo"] + spread_by, T.gg[:, :], T.wn[:, :].indirect(T.smo[:, :]))
     pick("scan", ["G"], T.sc, T.gg, W)
     ts("ob", ["scan", "ic"], T.ob[:, :], T.sc[:, 3:W:4], UP / 2048, ALU.mult, T.ic[:, 0:1], ALU.add)
-    ts("ci", ["scan"], T.ci[:, :], T.sc[:, 3:W:4], UP, ALU.mult)
+    ts("ci", ["scan"], T.ci[:, :], T.sc[:, 3:W:4], UP, ALU.mult, -1.0, ALU.add)
     ts("cl", ["ci"], T.cl[:, :], T.ci[:, :], 2047, ALU.bitwise_and)
-    ts("oa", ["cl", "ic4"], T.oa[:, :], T.cl[:, :], 4.0, ALU.mult, T.ic4[:, 0:1], ALU.add)
-    add("smr.0", ["smd.0", "ai"] + seq("wn", range(4)), lambda q: g.indirect_dma_start(T.smr[:, :], None, T.smd[:, :], IndirectOffsetOnAxis(ap=T.ai[:, 0:1], axis=0), bounds_check=3))
-    for b in range(4):
-        ts("oe%d" % b, ["smr.0", "ic"], T.oe[:, b:144:4], T.smr[:, 36 * b:36 * b + 36], 4.0, ALU.mult, T.ic[:, 0:1], ALU.add)
+    ts("oa", ["cl", "ic"], T.oa[:, :], T.cl[:, :], 4.0, ALU.mult, T.ic[:, 0:1], ALU.add)
+    add("smr.0", ["smd.0", "ai"] + [n for n in ORDER["g"][:ORDER["g"].index("sm0s")] if n[:2] in ("sg", "wn", "ho") and ORDER["g"].index(n) < (ORDER["g"] + ["smr.0"]).index("smr.0")], lambda q: g.indirect_dma_start(T.smr[:, :], None, T.smd[:, :], IndirectOffsetOnAxis(ap=T.ai[:, 0:1], axis=0), bounds_check=3))
+    oe = seq("oe", range(4))
+    if "smr.0" in ORDER["g"]:
+        for b in range(4):
+            ts("oe%d" % b, ["smr.0", "ic"], T.oe[:, b:144:4], T.smr[:, 36 * b:36 * b + 36], 4.0, ALU.mult, T.ic[:, 0:1], ALU.add)
+    else:
+        for k in range(8):
+            dma("smr.%d" % k, ["smd.0"], T.smr[16 * (k // 4) + k % 4:16 * (k // 4) + 16:4, :], T.smd[:, :])
+        for b in range(4):
+            ts("oe%d" % b, ["smr.0", "ic"], T.oe[0:32, b:144:4], T.smr[0:32, 36 * b:36 * b + 36], 4.0, ALU.mult, T.ic[0:32, 0:1], ALU.add)
+        copy("os1", oe, T.oe[32:64, :], T.oe[0:32, :])
+        copy("os2", ["os1"], T.oe[64:128, :], T.oe[0:64, :])
+        oe = ["os2"]
 
     for o, d in enumerate(blocks):
         gb, uu, zz = (T["%s%d" % (n, o)] for n in ("gb", "uu", "zz"))
         c = 36 * d
-        halves = (("a", 0, H), ("b", H, W))
-        for x, a, b in (("", 0, W),) + halves:
-            copy("B%d%s" % (o, x), pb_full + ["ob"], gb[:, a:b], T.pb[:, :].indirect(T.ob[:, c + a // 16:c + b // 16]))
-            add("R%d%s" % (o, x), ["E%d" % o], lambda q, out=T.mt[:, W * o + a:W * o + b], in_=zz[:, a:b]:
+
+        def over(step, a, b, o=o):
+            return [step + str(o) + x for x in PIECES if step + str(o) + x in listed and PIECES[x][0] < b and a < PIECES[x][1]]
+        for x, (a, b) in PIECES.items():
+            n, at = str(o) + x, slice(c + a // 16, c + b // 16)
+            copy("B" + n, pb_full + ["ob"], gb[:, a:b], T.pb[:, :].indirect(T.ob[:, at]))
+            tt("A" + n, pa_full + ["oa"] + over("B", a, b), uu[:, a:b], T.pa[:, :].indirect(T.oa[:, at]), gb[:, a:b], ALU.add)
+            tt("E" + n, ["e.0"] + oe + over("A", a, b), zz[:, a:b], T.eb[:, :].indirect(T.oe[:, at]), uu[:, a:b], ALU.add)
+            add("R" + n, over("E", a, b), lambda q, out=T.mt[:, W * o + a:W * o + b], in_=zz[:, a:b]:
                 A.activation(out, in_, ACT.Relu, scale=0.05) if q == "s" else V.tensor_scalar(out, in_, 0.0, 0.05, ALU.max, ALU.mult))
-        tt("A%d" % o, pa_full + ["oa", "B%d" % o], uu[:, :], T.pa[:, :].indirect(T.oa[:, c:c + 36]), gb[:, :], ALU.add)
-        tt("E%d" % o, ["e.0", "A%d" % o] + seq("oe", range(4)), zz[:, :], T.eb[:, :].indirect(T.oe[:, c:c + 36]), uu[:, :], ALU.add)
         here, there = slice(CM * o, CM * o + CM), slice(CM * r, CM * r + CM)
-        quant("Q%d" % o, ["R%d" % o], T.mmq[:, here], T.mmp[:, here], T.mt[:, W * o:W * o + W])
+        quant("Q%d" % o, over("R", 0, W), T.mmq[:, here], T.mmp[:, here], T.mt[:, W * o:W * o + W])
         if d != r:
             send("sm%ds" % o, ["Q%d" % o], d, "lme", "am%d" % r,
                  [(T.rrq[:, there].bitcast(dt.uint8), T.mmq[:, here].bitcast(dt.uint8)), (T.rrp[:, there], T.mmp[:, here])])
 
-    add("nlr.0", ["nld.0", "ii"], lambda q: g.indirect_dma_start(T.nlr[:, :], None, T.nld[:, :], IndirectOffsetOnAxis(ap=T.ii[:, 0:1], axis=0), bounds_check=3))
-    ts("nl1", ["nlr.0"], T.nmv[:, :], T.nlr[:, :], 2.0, ALU.add)
-    pick("nl2", ["nl1"], T.nsc, T.nmv, NT)
-    tt("nl3", ["nl2"], T.nt1[:, :], T.nsc[:, 3:128:4], T.nsc[:, 131:256:4], ALU.max)
-    tt("nl4", ["nl3"], T.nt2[:, :], T.nt1[:, 0:16], T.nt1[:, 16:32], ALU.max)
-    ts("nl5", ["nl2"], T.onl[:, 16:64], T.nsc[:, 67:256:4], UP, ALU.mult, WO - 2.0, ALU.add)
-    ts("nl6", ["nl4"], T.nt3[:, :], T.nt2[:, :], 1.5 / UP, ALU.is_lt, 1.0 / UP, ALU.mult)
-    tt("nl7", ["nl6"], T.nt4[:, :], T.nsc[:, 3:64:4], T.nt3[:, :], ALU.subtract)
-    ts("nl8", ["nl7"], T.onl[:, 0:16], T.nt4[:, :], UP, ALU.mult, WO - 2.0, ALU.add)
+    for k in range(8):
+        dma("nl.%d" % k, [], T.nlr[4 * k:4 * k + 4, :], T.nl[:, :])
+    ts("nl1", ["nl.0"], T.nmv[0:32, :], T.nlr[0:32, :], 2.0, ALU.add)
+    pick("nl2", ["nl1"], T.nsc, T.nmv, NT, 32)
+    tt("nl3", ["nl2"], T.nt1[0:32, :], T.nsc[0:32, 3:128:4], T.nsc[0:32, 131:256:4], ALU.max)
+    tt("nl4", ["nl3"], T.nt2[0:32, :], T.nt1[0:32, 0:16], T.nt1[0:32, 16:32], ALU.max)
+    ts("nl6", ["nl4"], T.nt3[0:32, :], T.nt2[0:32, :], 1.5 / UP, ALU.is_lt, 1.0 / UP, ALU.mult)
+    tt("nl7", ["nl6"], T.nsc[0:32, 3:64:4], T.nsc[0:32, 3:64:4], T.nt3[0:32, :], ALU.subtract)
+    for k, (a, b) in enumerate(((0, 32), (32, 64))):
+        ts("nl%d" % (8 + k), ["nl7"], T.onl[a:b, :], T.nsc[0:32, 3:256:4], UP, ALU.mult, WO - 2.0, ALU.add)
+    copy("on", ["nl8", "nl9"], T.onl[64:128, :], T.onl[0:64, :])
 
     for n, o in enumerate((0, 1, 3, 2)):
         s = blocks[o]
@@ -246,11 +288,9 @@ def rank_program(g, core, T, topo):
             dep, cq, cp = "Q%d" % o, T.mmq[:, CM * o:CM * o + CM], T.mmp[:, CM * o:CM * o + CM]
         else:
             dep, cq, cp = "am%d" % s, T.rrq[:, CM * s:CM * s + CM], T.rrp[:, CM * s:CM * s + CM]
-        bank = T.ps[:, 512 * n:512 * n + CM]
-        add("vP%d" % n, ["qv", dep, "mC%d" % n], lambda q, bank=bank, cq=cq, cp=cp: PE.matmul_mx(bank, T.vvq[:, :], T.vvp[:, :], cq, cp, True, True))
-        copy("vC%d" % n, ["vP%d" % n], T.win[:, WO + CM * s:WO + CM * s + CM], bank)
+        product("vP%d" % n, ["qv", dep], T.vvq[:, :], T.vvp[:, :], cq, cp, CM, T.win[:, WO + CM * s:WO + CM * s + CM])
 
-    ready = ["win0", "win1", "nl5", "nl8"] + seq("vC", range(4))
+    ready = ["win0", "win1", "on"] + seq("vC", range(4))
     for k, (x, a, b) in enumerate((("a", 0, NA), ("b", NA, NT))):
         steps = (T.g0, T.m1, T.m2, T.yb)
         for f in range(4):
@@ -262,7 +302,7 @@ def rank_program(g, core, T, topo):
         dma("y.%d" % k, ["y3" + x], T.y[:, a:b], T.yb[:, a:b])
 
     silent = ["go"] + [n for n in ORDER["g"] if n == "sn0" or n.endswith("s")]
-    total = {"go": 1}
+    total = {"go": 1} if "go" in ORDER["g"] else {}
     total.update(sent)
     for q in ORDER:
         for n in ORDER[q]:

@@ -1,14 +1,15 @@
 from concourse.mybir import dt, AluOpType, ActivationFunctionType
-from concourse.bass import IndirectOffsetOnAxis
+from concourse.bass import IndirectOffsetOnAxis, DstId, RemoteDMATransfer
 
 N, NT, E, CN, CM = 4, 256, 512, 128, 144
 NH = NT + N * CN
 WO = 8
-NA = 64
+NA = 128
 W, H = 4 * CM, 2 * CM
+C2 = H // 4
 UP = 2.0 ** 24
-PARTS = ((None, None), (None, None), (None, None))
-PIECES = {"": (0, W), "a": (0, H), "b": (H, W), "c": (H, H + CM), "d": (H + CM, W)}
+PIECES = {"": (0, W), "a": (0, H), "b": (H, W), "c": (H, H + CM), "d": (H + CM, W), "e": (0, W - 160), "f": (W - 160, W), "g": (0, 128), "h": (128, 256),
+          "i": (0, 256), "j": (256, W), "k": (256, W - 160)}
 ALU, ACT = AluOpType, ActivationFunctionType
 
 SCRATCH = {
@@ -17,30 +18,29 @@ SCRATCH = {
     "wab": ("sbuf", [128, 2048], "bfloat16"),
     "wbb": ("sbuf", [128, 2048], "bfloat16"),
     "vb": ("sbuf", [128, 512], "bfloat16"),
-    "ht": ("sbuf", [128, 4 * 3 * CN], "bfloat16"),
+    "ht": ("sbuf", [128, 4 * N * CN], "bfloat16"),
     "mt": ("sbuf", [128, 4 * N * CM], "bfloat16"),
     "pa": ("sbuf", [128, 4 * NH], "float32"),
     "pb": ("sbuf", [128, 4 * NH], "float32"),
     "smd": ("dram", [4, 144], "int32"),
     "ps": ("psum", [128, 4096], "float32"),
 }
-for _n, _w in (("snl", 32), ("sml", 36), ("eds", 64), ("nlr", 256), ("smr", 144), ("pi", 1), ("ai", 1), ("ii", 1), ("ci", 144), ("cl", 144),
-               ("rpi", 32)):
+for _n, _w in (("snl", 32), ("sml", 18), ("eds", 64), ("nlr", 256), ("smr", 144), ("pi", 1), ("ai", 1), ("ii", 1), ("ci", 144), ("cl", 144), ("rpi", 32)):
     SCRATCH[_n] = ("sbuf", [128, _w], "int32")
-for _n, _w in (("pk0", 16), ("pk", 16), ("wide", E), ("tr", 128), ("trt", 128), ("wn", E), ("af", 1), ("ic", 1), ("ic4", 1), ("j4", 4), ("w1", 4), ("w2", 4),
-               ("w4", 4), ("one", CM), ("wt", W), ("gg", W), ("sc", W), ("nmv", 256), ("nsc", 256), ("nt1", 32), ("nt2", 16), ("nt3", 16),
-               ("nt4", 16), ("win", WO + N * CM), ("g0", NT), ("m1", NT), ("m2", NT), ("yb", NT)):
+for _n, _w in (("pk0", 16), ("pk", 16), ("wide", E), ("tr", 128), ("trt", 128), ("wn", E), ("af", 1), ("ic", 1), ("j4", 4), ("w1", 4), ("w2", 4), ("w4", 4), ("one", C2), ("tiny", C2),
+               ("wt", H), ("gg", H), ("sc", H), ("nmv", 256), ("nsc", 256), ("nt1", 32), ("nt2", 16), ("nt3", 16),
+               ("win", WO + N * CM), ("g0", NT), ("m1", NT), ("m2", NT), ("yb", NT)):
     SCRATCH[_n] = ("sbuf", [128, _w], "float32")
-for _n, _w in (("rp", 32), ("smo", 36), ("oe", 144), ("oa", 144), ("ob", 144), ("onl", 64), ("oft0", 32), ("oft1", 32), ("oft2", 32), ("oft3", 32)):
+for _n, _w in (("rp", 32), ("smo", 18), ("oe", 144), ("oo", 288), ("oa", 144), ("ob", 144), ("onl", 64), ("oft0", 32), ("oft1", 32), ("oft2", 32), ("oft3", 32)):
     SCRATCH[_n] = ("sbuf", [128, _w], "uint16")
 for _k in range(4):
     for _n in ("gb", "uu", "zz"):
         SCRATCH["%s%d" % (_n, _k)] = ("sbuf", [128, W], "float32")
-for _n, _w in (("h", 3 * CN), ("nn", N * CN), ("xx", NT), ("wa", 512), ("wb", 512), ("vv", 128), ("mm", N * CM), ("rr", N * CM)):
+for _n, _w in (("h", N * CN), ("nn", N * CN), ("xx", NT), ("wa", 512), ("wb", 512), ("vv", 128), ("mm", N * CM), ("rr", N * CM)):
     SCRATCH[_n + "q"] = ("sbuf", [128, _w], "float8_e4m3fn_x4")
     SCRATCH[_n + "p"] = ("sbuf", [128, _w], "uint8")
 
-LOADS = ["sn", "x", "ed", "wa", "wb", "wl", "sm", "smd", "sg", "nl", "e", "v", "smr", "y", "ac0", "ac1", "ac2", "ac3"]
+LOADS = ["sn", "x", "ed", "wa", "wb", "sm", "smd", "nl", "e", "v", "smr", "ac0", "ac1", "on", "y"]
 SEMAPHORES = ["cv", "cs", "ct", "cg", "lno", "lme", "go"] + ["d_" + _n for _n in LOADS] + ["an%d" % _k for _k in range(4)] + ["am%d" % _k for _k in range(4)]
 
 
@@ -49,19 +49,20 @@ def seq(name, items):
 
 
 ORDER = {
-    "y": "sn.0 x.0 ed.0 ed.1 wb.0 sm.0 sm.1 sm.2 sm.3 sm.4 sm.5 sm.6 sm.7 smd.0 smd.1 smd.2 smd.3 nl.0 nl.1 nl.2 nl.3 nl.4 nl.5 nl.6 nl.7 e.0 v.0 y.0 y.1",
-    "s": "sn.1 x.1 ed.2 ed.3 wa.0 wt0 wt1 wt2 "
-         "n02 n03 n12 n13 n21 pk1 n22 pk2 n23 wide oC0 oC1 oC2 oC3 G oC4 oC6 "
-         "fC4 fC5 fC6 fC7 fC0 fC1 fC2 fC3 pC4 pC6 pC0 pC2 mC4 mC6 B0a mC1 mC3 "
-         "B1 B2 R0 R1 B3 R2a R2b R3a R3c vC0 vC1 vC3 y0b",
-    "v": "one win0 ai win1 af rp w1 w2 sn1 w4 sn2 ii of2 of3 of0 of1 "
-         "n00 n01 pk0 hq0 pk n10 n11 qx hq1 qa n20 smo hq2 wn qb nl1 wt3 ic oC5 nl2 oC7 nl3 scan nl4 "
-         "ci ob cl nl6 oa pC5 pC7 pC1 pC3 oe0 oe1 oe2 oe3 mC5 mC7 B0b mC0 mC2 nl7 "
-         "A0 A1 E0 E1 Q0 A2 Q1 E2a E2b A3a Q2 A3b qv E3a E3b nl8 R3d nl9 Q3 on vC2 "
+    "y": "sn.0 x.0 wb.0 " + " ".join(seq("ed.", range(6)) + seq("sm.", range(8)) + seq("nl.", range(8)) + seq("smd.", range(4)))
+         + " e.0 v.0 on.0 on.1 on.2 y.1",
+    "s": "sn.1 x.1 wa.0 ed.6 ed.7 wt0 wt1 wt2 wt3 "
+         "nf2 nf3 np2 np3 nm1 nm2 nm3 wide oC0 oC1 oC2 G oC4 oC6 "
+         "fC4 fC6 fC0 fC2 fC3 pC4 pC6 pC0 pC2 mC4 mC6 mC1 B0a mC3 "
+         "B1 oe0 oe1 oe2 oe3 B2 R0 win0 R1a R1b B3 R2e nl8 win1 R3i R3k vC0 vC1 vC3 y0b y.0",
+    "v": "one tiny ai ii af rp w1 w2 sn1 w4 sn2 ic of2 of3 of0 of1 "
+         "nf0 nf1 qx hqf np0 np1 qa hqp nm0 qb hqm smo wn oC3 oC5 oC7 scan nl2 "
+         "o0 o1 o2 o3 fC5 fC7 oaa fC1 nl3 oab pC5 pC7 pC1 pC3 nl4 mC5 mC7 mC0 B0b mC2 nl6 "
+         "A0 A1a E0 A1b E1a Q0 E1b A2 Q1 nl7 E2e E2f A3g R2f A3h Q2 A3j E3i E3j qv R3f Q3 vC2 "
          "y0a y1a y1b y2a y2b y3a y3b",
     "t": "oP0 oP1 oP2 oP3 oP4 oP5 oP6 oP7 fP4 fP5 fP6 fP7 fP0 fP1 fP2 fP3 pP4 pP5 pP6 pP7 pP0 pP1 pP2 pP3 "
          "mP4 mP5 mP6 mP7 mP0 mP1 mP2 mP3 vP0 vP1 vP3 vP2",
-    "g": "pi j4 rp0 holea sn0 sn1s sn2s smr.0 go holeb sm0s sm1s sm2s",
+    "g": "pi j4 rp0 holea sendf sendp sendm holeb go smr.0 send0 send1 send2",
 }
 ORDER = {_q: ORDER[_q].split() for _q in ORDER}
 
@@ -73,7 +74,6 @@ def rank_program(g, core, T, topo):
     S = T.sem
     Q = {"g": g, "v": g.vector, "s": g.scalar, "t": g.tensor, "y": g.sync}
     V, A, PE = g.vector, g.scalar, g.tensor
-    EARLY = 4 if "ql" not in ORDER["v"] else 3 if ORDER["t"].index("oP2") < 8 else 2
     listed = [n for q in ORDER for n in ORDER[q]]
     task = {}
     tok = {}
@@ -108,51 +108,50 @@ def rank_program(g, core, T, topo):
     def quant(name, deps, c, p, in_):
         add(name, deps, lambda q: V.quantize_mx(c, p, in_))
 
-    def pick(name, deps, out, in_, n, p=128):
+    def pick(name, deps, out, in_, n, p):
         add(name, deps + seq("wt", range(4)), lambda q: V.tensor_tensor_scan(out[0:p, :], in_[0:p, :], T.wt[0:p, 0:n], 0.0, ALU.max, ALU.mult))
 
     sent = {"lno": 0, "lme": 0}
 
-    def engines(src, dst, part):
-        e = topo.engines(src, dst)
-        return e if part is None else e[part * len(e) // 2:(part + 1) * len(e) // 2]
-
-    def send(name, deps, d, lsem, rsem, pairs, parts=(None, None)):
-        dst = T.cores[d]
-        rid, pid, _ = topo.addr(dst)
-        sent[lsem] += sum(len(engines(core, dst, p)) for p in parts)
+    def send(name, deps, ds, lsem, rsem, calls):
+        masks = []
+        for k, d in enumerate(ds):
+            e = topo.engines(core, T.cores[d])
+            masks.append(e[k * len(e) // len(ds):(k + 1) * len(e) // len(ds)])
+            sent[lsem] += len(calls) * len(masks[-1])
 
         def fn(q):
-            for (o, i), p in zip(pairs, parts):
-                g.remote_dma(o, i, S[rsem], S[lsem], pid, rid, sum(1 << e for e in engines(core, dst, p)))
+            for pairs in calls:
+                if len(ds) == 1:
+                    rid, pid, _ = topo.addr(T.cores[ds[0]])
+                    g.remote_dma(pairs[0][0], pairs[0][1], S[rsem], S[lsem], pid, rid, topo.mask(core, T.cores[ds[0]]))
+                else:
+                    g.remote_dma_fused([RemoteDMATransfer(dst_ids=[DstId(rid=topo.addr(T.cores[d])[0], pnc=topo.addr(T.cores[d])[1])], dma_engine_mask=sum(1 << e for e in m),
+                                                          remote_sem=S[rsem], src=i, dst=o) for d, m, (o, i) in zip(ds, masks, pairs)], local_sem=S[lsem])
         add(name, deps, fn)
 
     for o, s in enumerate(others):
-        tok["an%d" % s] = ("an%d" % s, sum(len(engines(T.cores[s], core, p)) for p in PARTS[o]))
-        tok["am%d" % s] = ("am%d" % s, 2 * len(topo.engines(T.cores[s], core)))
+        n = 2 * len(topo.engines(T.cores[s], core))
+        tok["an%d" % s] = ("an%d" % s, n // 2 if (o < 2 and "sendfp" in listed) or (o > 0 and "sendpm" in listed) else n)
+        tok["am%d" % s] = ("am%d" % s, n)
 
-    def spread(name, dep, t):
-        copy(name + "1", [dep], t[32:64, :], t[0:32, :])
-        copy(name + "2", [name + "1"], t[64:128, :], t[0:64, :])
-
-    for k in range(8):
-        dma("sn.%d" % k, [], T.snl[16 * k:16 * k + 16, :], T.sn[:, :])
     for k in range(2):
+        dma("sn.%d" % k, [], T.snl[16 * k:16 * k + 16, :], T.sn[:, :])
         dma("x.%d" % k, [], T.xb[64 * k:64 * k + 64, :], T.x[64 * k:64 * k + 64, :])
     for k in range(8):
-        dma("sm.%d" % k, [], T.sml[16 * k:16 * k + 16, :], T.sm[:, :])
+        dma("sm.%d" % k, [], T.sml[16 * k:16 * k + 16, :], T.sm[:, 18 * (k // 4):18 * (k // 4) + 18])
     for h in range(2):
         dma("ed.%d" % h, [], T.eds[16 * h:16 * h + 16, 0:31], T.es[:, h:h + 31])
         dma("ed.%d" % (h + 2), [], T.eds[16 * h:16 * h + 16, 32:63], T.ed[:, h:h + 31])
-    dma("wa.0", [], T.wab[:, 0:512 * EARLY], T.wa[:, 0:512 * EARLY])
-    if EARLY < 4:
-        dma("wl.0", ["go"], T.wab[:, 512 * EARLY:2048], T.wa[:, 512 * EARLY:2048])
-        quant("ql", ["wl.0"], T.waq[:, 128 * EARLY:512], T.wap[:, 128 * EARLY:512], T.wab[:, 512 * EARLY:2048])
+    if "oab" in listed:
+        for k in range(8):
+            dma("sm.%d" % k, [], T.sml[16 * k:16 * k + 16, :], T.sm[:, 18 * (k // 2 % 2):18 * (k // 2 % 2) + 18])
+            dma("ed.%d" % k, [], T.eds[16 * k:16 * k + 16, 0:31], (T.es if k < 4 else T.ed)[:, k % 2:k % 2 + 31])
+    dma("wa.0", [], T.wab[:, :], T.wa[:, :])
     dma("wb.0", [], T.wbb[:, :], T.wb[:, :])
     for a in range(4):
         dma("smd.%d" % a, [], T.smd[a:a + 1, :], T.sm[a:16:4, :])
-        dma("sg.%d" % a, [], T.smd[a:a + 1, :], T.sm[a:16:4, :])
-    dma("e.0", ["go"] if "go" in ORDER["g"] else [], T.eb[:, :], T.e[:, :])
+    dma("e.0", ["go"], T.eb[:, :], T.e[:, :])
     dma("v.0", [], T.vb[:, :], T.v[:, :])
     add("go", [], lambda q: g.sem_inc(S.go, 1))
     tok["go"] = ("go", 1)
@@ -160,8 +159,12 @@ def rank_program(g, core, T, topo):
     add("pi", [], lambda q: g.iota(T.pi[:, :], [[0, 1]], 0, 1))
     add("j4", [], lambda q: g.iota(T.j4[:, :], [[1, 4]], 0, 0, allow_small_or_imprecise_dtypes=True))
     fill("one", T.one[:, :], 1.0)
-    fill("win0", T.win[:, 0:WO - 1], 0.0)
-    fill("win1", T.win[:, WO - 1:WO], -1e29)
+    fill("pad", T.tr[:, :], 0.0)
+    for n, a, b, c in (("win0", 0, WO - 1, 0.0), ("win1", WO - 1, WO, -1e29)):
+        if n in ORDER["v"]:
+            fill(n, T.win[:, a:b], c)
+        else:
+            add(n, ["one"], lambda q, a=a, b=b, c=c: A.activation(T.win[:, a:b], T.one[:, a:b], ACT.Identity, scale=c))
     ts("ai", ["pi"], T.ai[:, :], T.pi[:, :], 2, ALU.logical_shift_right, 3, ALU.bitwise_and)
     ts("ii", ["pi"], T.ii[:, :], T.pi[:, :], 3, ALU.bitwise_and)
     copy("af", ["ai"], T.af[:, :], T.ai[:, :])
@@ -170,38 +173,51 @@ def rank_program(g, core, T, topo):
     ts("w2", ["af", "j4"], T.w2[:, :], T.j4[:, :], T.af[:, 0:1], ALU.is_gt)
     tt("w4", ["w1", "w2"], T.w4[:, :], T.w1[:, :], T.w2[:, :], ALU.add)
     for m in range(3):
-        add("wt%d" % m, ["one", "w4"], lambda q, m=m: A.activation(T.wt[:, m:W:4], T.one[:, :], ACT.Identity, scale=T.w4[:, m:m + 1]))
-    ts("wt3", ["one", "w4"], T.wt[:, 3:W:4], T.one[:, :], T.w4[:, 3:4], ALU.mult, UP ** -2, ALU.mult)
+        add("wt%d" % m, ["one", "w4"], lambda q, m=m: A.activation(T.wt[:, m:H:4], T.one[:, :], ACT.Identity, scale=T.w4[:, m:m + 1]))
+    fill("tiny", T.tiny[:, :], UP ** -2)
+    if "tiny" in listed:
+        add("wt3", ["tiny", "w4"], lambda q: A.activation(T.wt[:, 3:H:4], T.tiny[:, :], ACT.Identity, scale=T.w4[:, 3:4]))
+    else:
+        ts("wt3", ["one", "w4"], T.wt[:, 3:H:4], T.one[:, :], T.w4[:, 3:4], ALU.mult, UP ** -2, ALU.mult)
     hole = 4 * (NT + CN * r)
     fill("holea", T.pa[:, hole:hole + 4 * CN], 0.0)
-    if "holeb" not in ORDER["s"]:
-        fill("holeb", T.pb[:, hole:hole + 4 * CN], 0.0)
-    else:
-        copy("holeb", ["holea"], T.pb[:, hole:hole + 4 * CN], T.pa[:, hole:hole + 4 * CN])
+    fill("holeb", T.pb[:, hole:hole + 4 * CN], 0.0)
 
-    spread("sn", "sn.0", T.snl)
+    copy("sn1", ["sn.0"], T.snl[32:64, :], T.snl[0:32, :])
+    copy("sn2", ["sn1"], T.snl[64:128, :], T.snl[0:64, :])
+    for k in range(1, 4):
+        copy("sq%d" % k, ["sn.0"], T.snl[32 * k:32 * k + 32, :], T.snl[0:32, :])
     for t in range(4):
-        ts("of%d" % t, ["sn2" if "sn2" in listed else "sn.0"], T["oft%d" % t][:, :], T.snl[:, :], 4.0, ALU.mult, float(t), ALU.add)
-    for o, d in enumerate(others):
+        ts("of%d" % t, ["sn2"] if "sn2" in listed else seq("sq", range(1, 4)), T["oft%d" % t][:, :], T.snl[:, :], 4.0, ALU.mult, float(t), ALU.add)
+    groups = {"f": others[:1], "p": others[1:2], "d": others[:2], "m": others[2:]}
+    assert max(groups["d"]) == min(groups["d"]) + 1
+    for x in groups:
+        d, n = min(groups[x]), len(groups[x])
         for t in range(4):
-            copy("n%d%d" % (o, t), ["x.0", "of%d" % t], T.ht[:, 512 * o + t:512 * o + 512:4], T.xb[:, :].indirect(T["oft%d" % t][:, 8 * d:8 * d + 8]))
-        here, there = slice(CN * o, CN * o + CN), slice(CN * r, CN * r + CN)
-        quant("hq%d" % o, seq("n%d" % o, range(4)), T.hq[:, here], T.hp[:, here], T.ht[:, 512 * o:512 * o + 512])
-        send(("sn0", "sn1s", "sn2s")[o], ["hq%d" % o], d, "lno", "an%d" % r,
-             [(T.nnq[:, there].bitcast(dt.uint8), T.hq[:, here].bitcast(dt.uint8)), (T.nnp[:, there], T.hp[:, here])], PARTS[o])
+            copy("n%s%d" % (x, t), ["x.0", "of%d" % t], T.ht[:, 512 * d + t:512 * (d + n):4], T.xb[:, :].indirect(T["oft%d" % t][:, 8 * d:8 * (d + n)]))
+        quant("hq" + x, seq("n" + x, range(4)), T.hq[:, CN * d:CN * (d + n)], T.hp[:, CN * d:CN * (d + n)], T.ht[:, 512 * d:512 * (d + n)])
+    there = slice(CN * r, CN * r + CN)
+    for x in ("f", "p", "m", "fp", "pm"):
+        ds = [groups[c][0] for c in x]
+        if "send" + x in listed:
+            send("send" + x, ["hq" + c if "hq" + c in listed else "hqd" for c in x], ds, "lno", "an%d" % r,
+                 [[(T.nnq[:, there].bitcast(dt.uint8), T.hq[:, CN * c:CN * c + CN].bitcast(dt.uint8)) for c in ds],
+                  [(T.nnp[:, there], T.hp[:, CN * c:CN * c + CN]) for c in ds]])
 
-    quant("qa", ["wa.0"], T.waq[:, 0:128 * EARLY], T.wap[:, 0:128 * EARLY], T.wab[:, 0:512 * EARLY])
+    quant("qa", ["wa.0"], T.waq[:, :], T.wap[:, :], T.wab[:, :])
     quant("qb", ["wb.0"], T.wbq[:, :], T.wbp[:, :], T.wbb[:, :])
+    for h in range(2):
+        quant("qa%d" % h, ["wa.0"], T.waq[:, 256 * h:256 * h + 256], T.wap[:, 256 * h:256 * h + 256], T.wab[:, 1024 * h:1024 * h + 1024])
+        quant("qb%d" % h, ["wb.0"], T.wbq[:, 256 * h:256 * h + 256], T.wbp[:, 256 * h:256 * h + 256], T.wbb[:, 1024 * h:1024 * h + 1024])
     quant("qx", ["x.0"], T.xxq[:, :], T.xxp[:, :], T.xb[:, :])
     quant("qv", ["v.0"], T.vvq[:, :], T.vvp[:, :], T.vb[:, :])
+
     def product(name, deps, wq, wp, cq, cp, n, out):
         k = ORDER["t"].index(name)
         bank = T.ps[:, 512 * (k % 8):512 * (k % 8) + n]
         add(name, deps + [x.replace("P", "C") for x in ORDER["t"][max(k - 8, 0):max(k - 7, 0)]], lambda q: PE.matmul_mx(bank, wq, wp, cq, cp, True, True))
         copy(name.replace("P", "C"), [name], out, bank)
 
-    groups = {"f": others[:1], "p": others[1:2], "d": others[:2], "m": others[2:]}
-    assert max(groups["d"]) == min(groups["d"]) + 1
     pa_full, pb_full = ["holea"], ["holeb"]
     for name in ORDER["t"]:
         j = int(name[2])
@@ -212,44 +228,53 @@ def rank_program(g, core, T, topo):
             deps, cq, cp, h = seq("an", groups[name[0]]), T.nnq[:, c:c + n], T.nnp[:, c:c + n], NT + c
         else:
             continue
-        c, p, w, win, full = (T.waq, T.wap, "qa" if j < EARLY else "ql", T.pa, pa_full) if j < 4 else (T.wbq, T.wbp, "qb", T.pb, pb_full)
+        c, p, w, win, full = (T.waq, T.wap, "qa", T.pa, pa_full) if j < 4 else (T.wbq, T.wbp, "qb", T.pb, pb_full)
         b = slice(128 * (j % 4), 128 * (j % 4) + 128)
-        product(name, deps + [w], c[:, b], p[:, b], cq, cp, n, win[:, 4 * h + j % 4:4 * h + 4 * n:4])
+        product(name, deps + [w if w in listed else w + str(j % 4 // 2)], c[:, b], p[:, b], cq, cp, n, win[:, 4 * h + j % 4:4 * h + 4 * n:4])
         full.append(name.replace("P", "C"))
 
     ts("pk0", ["ed.0"], T.pk0[0:32, :], T.eds[0:32, 32:63:2], 8192.0, ALU.mult, 1.0, ALU.add)
+    for a in range(4):
+        tt("pq%d" % a, ["pk0", "pad"], T.tr[32 * a:32 * a + 32, 0:128:32], T.eds[0:32, 8 * a:8 * a + 7:2], T.pk0[0:32, 4 * a:4 * a + 4], ALU.add)
+        add("wn%d" % a, ["trp"], lambda q, a=a: g.partition_broadcast(T.wn[:, 128 * a:128 * a + 128], T.trt[32 * a:32 * a + 1, :], 128))
+    add("trp", seq("pq", range(4)), lambda q: V.transpose(T.trt[:, :], T.tr[:, :]))
     tt("pk", ["pk0"], T.pk[0:32, :], T.eds[0:32, 0:31:2], T.pk0[0:32, :], ALU.add)
-    spread("pk", "pk", T.pk)
+    copy("pk1", ["pk"], T.pk[32:64, :], T.pk[0:32, :])
+    copy("pk2", ["pk1"], T.pk[64:128, :], T.pk[0:64, :])
     add("rp0", [], lambda q: g.iota(T.rpi[:, :], [[1, 16], [0, 2]], 0, 0))
     copy("rp", ["rp0"], T.rp[:, :], T.rpi[:, :])
     copy("wide", ["pk2", "rp"], T.wide[:, :], T.pk[:, :].indirect(T.rp[:, :]))
     add("wn", ["wide"], lambda q: V.transpose(T.wn[:, :], T.wide[:, :]))
+    spread = ["wn"] if "wn" in listed else seq("wn", range(4))
     copy("smo", ["sm.0"], T.smo[:, :], T.sml[:, :])
-    fill("tz", T.tr[:, :], 0.0)
-    for a in range(4):
-        tt("pq%d" % a, ["pk0", "tz"], T.tr[32 * a:32 * a + 32, 0:128:32], T.eds[0:32, 8 * a:8 * a + 7:2], T.pk0[0:32, 4 * a:4 * a + 4], ALU.add)
-        add("wn%d" % a, ["trp"], lambda q, a=a: g.partition_broadcast(T.wn[:, 128 * a:128 * a + 128], T.trt[32 * a:32 * a + 1, :], 128))
-    add("trp", seq("pq", range(4)), lambda q: V.transpose(T.trt[:, :], T.tr[:, :]))
-    spread_by = ["wn"] if "wn" in listed else seq("wn", range(4))
-    copy("G", ["smo"] + spread_by, T.gg[:, :], T.wn[:, :].indirect(T.smo[:, :]))
-    pick("scan", ["G"], T.sc, T.gg, W)
-    ts("ob", ["scan", "ic"], T.ob[:, :], T.sc[:, 3:W:4], UP / 2048, ALU.mult, T.ic[:, 0:1], ALU.add)
-    ts("ci", ["scan"], T.ci[:, :], T.sc[:, 3:W:4], UP, ALU.mult, -1.0, ALU.add)
-    ts("cl", ["ci"], T.cl[:, :], T.ci[:, :], 2047, ALU.bitwise_and)
+    copy("G", ["smo"] + spread, T.gg[:, :], T.wn[:, :].indirect(T.smo[:, :]))
+    pick("scan", ["G"], T.sc, T.gg, H, 128)
+    for k in range(2):
+        h = blocks[2 * k] // 2
+        at = slice(C2 * h, C2 * h + C2)
+        for u in range(2):
+            ts("ci%d%d" % (k, u), ["scan"], T.ci[64 * u:64 * u + 64, at], T.sc[64 * h:64 * h + 64, 3:H:4], UP, ALU.mult, -1.0, ALU.add)
+        both = ["ci%d0" % k, "ci%d1" % k]
+        ts("ob%d" % k, both + ["ic"], T.ob[:, at], T.ci[:, at], 1.0 / 2048, ALU.mult, T.ic[:, 0:1], ALU.add)
+        ts("cl%d" % k, both, T.cl[:, at], T.ci[:, at], 2047, ALU.bitwise_and)
+        ts("oa%d" % k, ["cl%d" % k, "ic"], T.oa[:, at], T.cl[:, at], 4.0, ALU.mult, T.ic[:, 0:1], ALU.add)
+    four = ["ci00", "ci01", "ci10", "ci11"]
+    ts("ob", four + ["ic"], T.ob[:, :], T.ci[:, :], 1.0 / 2048, ALU.mult, T.ic[:, 0:1], ALU.add)
+    ts("cl", four, T.cl[:, :], T.ci[:, :], 2047, ALU.bitwise_and)
     ts("oa", ["cl", "ic"], T.oa[:, :], T.cl[:, :], 4.0, ALU.mult, T.ic[:, 0:1], ALU.add)
-    add("smr.0", ["smd.0", "ai"] + [n for n in ORDER["g"][:ORDER["g"].index("sm0s")] if n[:2] in ("sg", "wn", "ho") and ORDER["g"].index(n) < (ORDER["g"] + ["smr.0"]).index("smr.0")], lambda q: g.indirect_dma_start(T.smr[:, :], None, T.smd[:, :], IndirectOffsetOnAxis(ap=T.ai[:, 0:1], axis=0), bounds_check=3))
+    if "oab" in listed:
+        add("rp0", [], lambda q: g.iota(T.rpi[:, :], [[2, 16], [0, 2]], 0, 0))
+        copy("wide", ["ed.0", "rp"], T.wide[:, :], T.eds[:, 0:31].indirect(T.rp[:, :]))
+        add("scan", ["G"] + seq("wt", range(4)), lambda q: V.tensor_tensor_scan(T.sc[:, :], T.gg[:, :], T.wt[:, :], 0.0, ALU.add, ALU.mult))
+        for c in range(4):
+            ts("o%d" % c, ["scan", "ic"], T.oo[0:32, C2 * c:C2 * c + C2], T.sc[32 * c:32 * c + 32, 3:H:4], 4 * UP, ALU.mult, T.ic[32 * c:32 * c + 32, 0:1], ALU.add)
+        copy("oaa", seq("o", range(4)), T.oo[32:64, :], T.oo[0:32, :])
+        copy("oab", ["oaa"], T.oo[64:128, :], T.oo[0:64, :])
+    add("smr.0", ["smd.0", "ai"] + [n for n in ORDER["g"][:ORDER["g"].index("smr.0")] if n[:2] in ("wn", "ho")], lambda q: g.indirect_dma_start(T.smr[:, :], None, T.smd[:, :], IndirectOffsetOnAxis(ap=T.ai[:, 0:1], axis=0), bounds_check=3))
     oe = seq("oe", range(4))
-    if "smr.0" in ORDER["g"]:
-        for b in range(4):
-            ts("oe%d" % b, ["smr.0", "ic"], T.oe[:, b:144:4], T.smr[:, 36 * b:36 * b + 36], 4.0, ALU.mult, T.ic[:, 0:1], ALU.add)
-    else:
-        for k in range(8):
-            dma("smr.%d" % k, ["smd.0"], T.smr[16 * (k // 4) + k % 4:16 * (k // 4) + 16:4, :], T.smd[:, :])
-        for b in range(4):
-            ts("oe%d" % b, ["smr.0", "ic"], T.oe[0:32, b:144:4], T.smr[0:32, 36 * b:36 * b + 36], 4.0, ALU.mult, T.ic[0:32, 0:1], ALU.add)
-        copy("os1", oe, T.oe[32:64, :], T.oe[0:32, :])
-        copy("os2", ["os1"], T.oe[64:128, :], T.oe[0:64, :])
-        oe = ["os2"]
+    for b in range(4):
+        add("oe%d" % b, ["smr.0", "ic"], lambda q, out=T.oe[:, b:144:4], in_=T.smr[:, 36 * b:36 * b + 36]:
+            A.activation(out, in_, ACT.Identity, bias=T.ic[:, 0:1], scale=4.0) if q == "s" else V.tensor_scalar(out, in_, 4.0, T.ic[:, 0:1], ALU.mult, ALU.add))
 
     for o, d in enumerate(blocks):
         gb, uu, zz = (T["%s%d" % (n, o)] for n in ("gb", "uu", "zz"))
@@ -259,28 +284,38 @@ def rank_program(g, core, T, topo):
             return [step + str(o) + x for x in PIECES if step + str(o) + x in listed and PIECES[x][0] < b and a < PIECES[x][1]]
         for x, (a, b) in PIECES.items():
             n, at = str(o) + x, slice(c + a // 16, c + b // 16)
-            copy("B" + n, pb_full + ["ob"], gb[:, a:b], T.pb[:, :].indirect(T.ob[:, at]))
-            tt("A" + n, pa_full + ["oa"] + over("B", a, b), uu[:, a:b], T.pa[:, :].indirect(T.oa[:, at]), gb[:, a:b], ALU.add)
+            copy("B" + n, pb_full + ["ob" if "ob" in listed else "ob%d" % (o // 2)], gb[:, a:b], T.pb[:, :].indirect(T.ob[:, at]))
+            tt("A" + n, pa_full + ["oa" if "oa" in listed else "oa%d" % (o // 2)] + over("B", a, b), uu[:, a:b], T.pa[:, :].indirect(T.oa[:, at]), gb[:, a:b], ALU.add)
             tt("E" + n, ["e.0"] + oe + over("A", a, b), zz[:, a:b], T.eb[:, :].indirect(T.oe[:, at]), uu[:, a:b], ALU.add)
-            add("R" + n, over("E", a, b), lambda q, out=T.mt[:, W * o + a:W * o + b], in_=zz[:, a:b]:
+            if "oab" in listed:
+                copy("B" + n, pb_full + ["oab"], gb[:, a:b], T.pb[:, :].indirect(T.oo[:, CM + c + a // 16:CM + c + b // 16]))
+                tt("A" + n, pa_full + ["oab"] + over("B", a, b), uu[:, a:b], T.pa[:, :].indirect(T.oo[:, at]), gb[:, a:b], ALU.add)
+            copy("F" + n, ["e.0"] + oe, zz[:, a:b], T.eb[:, :].indirect(T.oe[:, at]))
+            added = "ac%d.0" % o in listed
+            add("R" + n, ["ac%d.0" % o] if added else over("E", a, b), lambda q, out=T.mt[:, W * o + a:W * o + b], in_=(uu if added else zz)[:, a:b]:
                 A.activation(out, in_, ACT.Relu, scale=0.05) if q == "s" else V.tensor_scalar(out, in_, 0.0, 0.05, ALU.max, ALU.mult))
+        add("ac%d.0" % o, over("A", 0, W) + over("F", 0, W), lambda q, uu=uu, zz=zz: g.dma_start(uu[:, :], zz[:, :], accum_op=ALU.add))
         here, there = slice(CM * o, CM * o + CM), slice(CM * r, CM * r + CM)
         quant("Q%d" % o, over("R", 0, W), T.mmq[:, here], T.mmp[:, here], T.mt[:, W * o:W * o + W])
         if d != r:
-            send("sm%ds" % o, ["Q%d" % o], d, "lme", "am%d" % r,
-                 [(T.rrq[:, there].bitcast(dt.uint8), T.mmq[:, here].bitcast(dt.uint8)), (T.rrp[:, there], T.mmp[:, here])])
+            send("send%d" % o, ["Q%d" % o], [d], "lme", "am%d" % r,
+                 [[(T.rrq[:, there].bitcast(dt.uint8), T.mmq[:, here].bitcast(dt.uint8))], [(T.rrp[:, there], T.mmp[:, here])]])
 
     for k in range(8):
         dma("nl.%d" % k, [], T.nlr[4 * k:4 * k + 4, :], T.nl[:, :])
-    ts("nl1", ["nl.0"], T.nmv[0:32, :], T.nlr[0:32, :], 2.0, ALU.add)
-    pick("nl2", ["nl1"], T.nsc, T.nmv, NT, 32)
+    copy("nl1", ["nl.0"], T.nmv[0:32, :], T.nlr[0:32, :])
+    add("nl2", ["nl1" if "nl1" in listed else "nl.0"] + seq("wt", range(4)),
+        lambda q: V.tensor_tensor_scan(T.nsc[0:32, :], (T.nmv if "nl1" in listed else T.nlr)[0:32, :], T.wt[0:32, 0:NT], 0.0, ALU.add, ALU.mult))
     tt("nl3", ["nl2"], T.nt1[0:32, :], T.nsc[0:32, 3:128:4], T.nsc[0:32, 131:256:4], ALU.max)
     tt("nl4", ["nl3"], T.nt2[0:32, :], T.nt1[0:32, 0:16], T.nt1[0:32, 16:32], ALU.max)
-    ts("nl6", ["nl4"], T.nt3[0:32, :], T.nt2[0:32, :], 1.5 / UP, ALU.is_lt, 1.0 / UP, ALU.mult)
+    ts("nl6", ["nl4"], T.nt3[0:32, :], T.nt2[0:32, :], -0.5 / UP, ALU.is_lt, 1.0 / UP, ALU.mult)
     tt("nl7", ["nl6"], T.nsc[0:32, 3:64:4], T.nsc[0:32, 3:64:4], T.nt3[0:32, :], ALU.subtract)
     for k, (a, b) in enumerate(((0, 32), (32, 64))):
-        ts("nl%d" % (8 + k), ["nl7"], T.onl[a:b, :], T.nsc[0:32, 3:256:4], UP, ALU.mult, WO - 2.0, ALU.add)
+        add("nl%d" % (8 + k), ["nl7"], lambda q, out=T.onl[a:b, :], in_=T.nsc[0:32, 3:256:4]:
+            A.activation(out, in_, ACT.Identity, bias=float(WO), scale=UP) if q == "s" else V.tensor_scalar(out, in_, UP, float(WO), ALU.mult, ALU.add))
     copy("on", ["nl8", "nl9"], T.onl[64:128, :], T.onl[0:64, :])
+    for k in range(3):
+        dma("on.%d" % k, ["nl8"], T.onl[32 * k + 32:32 * k + 64, :], T.onl[0:32, :])
 
     for n, o in enumerate((0, 1, 3, 2)):
         s = blocks[o]
@@ -290,7 +325,7 @@ def rank_program(g, core, T, topo):
             dep, cq, cp = "am%d" % s, T.rrq[:, CM * s:CM * s + CM], T.rrp[:, CM * s:CM * s + CM]
         product("vP%d" % n, ["qv", dep], T.vvq[:, :], T.vvp[:, :], cq, cp, CM, T.win[:, WO + CM * s:WO + CM * s + CM])
 
-    ready = ["win0", "win1", "on"] + seq("vC", range(4))
+    ready = ["win0", "win1", "on" if "on" in listed else "on.0"] + seq("vC", range(4))
     for k, (x, a, b) in enumerate((("a", 0, NA), ("b", NA, NT))):
         steps = (T.g0, T.m1, T.m2, T.yb)
         for f in range(4):
@@ -301,8 +336,8 @@ def rank_program(g, core, T, topo):
                 tt("y%d%s" % (f, x), ready + ["y%d%s" % (f - 1, x)], steps[f][:, a:b], at, steps[f - 1][:, a:b], ALU.max)
         dma("y.%d" % k, ["y3" + x], T.y[:, a:b], T.yb[:, a:b])
 
-    silent = ["go"] + [n for n in ORDER["g"] if n == "sn0" or n.endswith("s")]
-    total = {"go": 1} if "go" in ORDER["g"] else {}
+    silent = ["go"] + [n for n in ORDER["g"] if n.startswith("send")]
+    total = {"go": 1}
     total.update(sent)
     for q in ORDER:
         for n in ORDER[q]:
@@ -327,7 +362,7 @@ def rank_program(g, core, T, topo):
     for q in ORDER:
         for n in ORDER[q]:
             deps, fn = task[n]
-            need(q, [tok[x] for d in deps for x in ([d] if d in tok else [d + "a", d + "b"])])
+            need(q, [tok[d] for d in deps])
             ins = fn(q)
             if n not in silent:
                 ins.then_inc(S[tok[n][0]], 16 if "." in n else 1)

from concourse.mybir import dt, AluOpType, ActivationFunctionType
from concourse.bass import IndirectOffsetOnAxis, DstId, RemoteDMATransfer

N, NT, E, CN, CM = 4, 256, 512, 128, 144
NH = NT + N * CN
WO = 8
NA = 128
W, H = 4 * CM, 2 * CM
C2 = H // 4
UP = 2.0 ** 24
PIECES = {"": (0, W), "a": (0, H), "b": (H, W), "c": (H, H + CM), "d": (H + CM, W), "e": (0, W - 160), "f": (W - 160, W), "g": (0, 128), "h": (128, 256),
          "i": (0, 256), "j": (256, W), "k": (256, W - 160)}
ALU, ACT = AluOpType, ActivationFunctionType

SCRATCH = {
    "xb": ("sbuf", [128, 4 * NT], "bfloat16"),
    "eb": ("sbuf", [128, 4 * E], "bfloat16"),
    "wab": ("sbuf", [128, 2048], "bfloat16"),
    "wbb": ("sbuf", [128, 2048], "bfloat16"),
    "vb": ("sbuf", [128, 512], "bfloat16"),
    "ht": ("sbuf", [128, 4 * N * CN], "bfloat16"),
    "mt": ("sbuf", [128, 4 * N * CM], "bfloat16"),
    "pa": ("sbuf", [128, 4 * NH], "float32"),
    "pb": ("sbuf", [128, 4 * NH], "float32"),
    "smd": ("dram", [4, 144], "int32"),
    "ps": ("psum", [128, 4096], "float32"),
}
for _n, _w in (("snl", 32), ("sml", 18), ("eds", 64), ("nlr", 256), ("smr", 144), ("pi", 1), ("ai", 1), ("ii", 1), ("ci", 144), ("cl", 144), ("rpi", 32)):
    SCRATCH[_n] = ("sbuf", [128, _w], "int32")
for _n, _w in (("pk0", 16), ("pk", 16), ("wide", E), ("tr", 128), ("trt", 128), ("wn", E), ("af", 1), ("ic", 1), ("j4", 4), ("w1", 4), ("w2", 4), ("w4", 4), ("one", C2), ("tiny", C2),
               ("wt", H), ("gg", H), ("sc", H), ("nmv", 256), ("nsc", 256), ("nt1", 32), ("nt2", 16), ("nt3", 16),
               ("win", WO + N * CM), ("g0", NT), ("m1", NT), ("m2", NT), ("yb", NT)):
    SCRATCH[_n] = ("sbuf", [128, _w], "float32")
for _n, _w in (("rp", 32), ("smo", 18), ("oe", 144), ("oo", 288), ("oa", 144), ("ob", 144), ("onl", 64), ("oft0", 32), ("oft1", 32), ("oft2", 32), ("oft3", 32)):
    SCRATCH[_n] = ("sbuf", [128, _w], "uint16")
for _k in range(4):
    for _n in ("gb", "uu", "zz"):
        SCRATCH["%s%d" % (_n, _k)] = ("sbuf", [128, W], "float32")
for _n, _w in (("h", N * CN), ("nn", N * CN), ("xx", NT), ("wa", 512), ("wb", 512), ("vv", 128), ("mm", N * CM), ("rr", N * CM)):
    SCRATCH[_n + "q"] = ("sbuf", [128, _w], "float8_e4m3fn_x4")
    SCRATCH[_n + "p"] = ("sbuf", [128, _w], "uint8")

LOADS = ["sn", "x", "ed", "wa", "wb", "sm", "smd", "nl", "e", "v", "smr", "ac0", "ac1", "on", "y"]
SEMAPHORES = ["cv", "cs", "ct", "cg", "lno", "lme", "go"] + ["d_" + _n for _n in LOADS] + ["an%d" % _k for _k in range(4)] + ["am%d" % _k for _k in range(4)]


def seq(name, items):
    return [name + str(i) for i in items]


ORDER = {
    "y": "sn.0 x.0 wb.0 " + " ".join(seq("ed.", range(6)) + seq("sm.", range(8)) + seq("nl.", range(8)) + seq("smd.", range(4)))
         + " e.0 v.0 on.0 on.1 on.2 y.1",
    "s": "sn.1 x.1 wa.0 ed.6 ed.7 wt0 wt1 wt2 wt3 "
         "nf2 nf3 np2 np3 nm1 nm2 nm3 wide oC0 oC1 oC2 G oC4 oC6 "
         "fC4 fC6 fC0 fC2 fC3 pC4 pC6 pC0 pC2 mC4 mC6 mC1 B0a mC3 "
         "B1 oe0 oe1 oe2 oe3 B2 R0 win0 R1a R1b B3 R2e nl8 win1 R3i R3k vC0 vC1 vC3 y0b y.0",
    "v": "one tiny ai ii af rp w1 w2 sn1 w4 sn2 ic of2 of3 of0 of1 "
         "nf0 nf1 qx hqf np0 np1 qa hqp nm0 qb hqm smo wn oC3 oC5 oC7 scan nl2 "
         "o0 o1 o2 o3 fC5 fC7 oaa fC1 nl3 oab pC5 pC7 pC1 pC3 nl4 mC5 mC7 mC0 B0b mC2 nl6 "
         "A0 A1a E0 A1b E1a Q0 E1b A2 Q1 nl7 E2e E2f A3g R2f A3h Q2 A3j E3i E3j qv R3f Q3 vC2 "
         "y0a y1a y1b y2a y2b y3a y3b",
    "t": "oP0 oP1 oP2 oP3 oP4 oP5 oP6 oP7 fP4 fP5 fP6 fP7 fP0 fP1 fP2 fP3 pP4 pP5 pP6 pP7 pP0 pP1 pP2 pP3 "
         "mP4 mP5 mP6 mP7 mP0 mP1 mP2 mP3 vP0 vP1 vP3 vP2",
    "g": "pi j4 rp0 holea sendf sendp sendm holeb go smr.0 send0 send1 send2",
}
ORDER = {_q: ORDER[_q].split() for _q in ORDER}


def rank_program(g, core, T, topo):
    r = T.rank_of(core)
    if r is None:
        return
    S = T.sem
    Q = {"g": g, "v": g.vector, "s": g.scalar, "t": g.tensor, "y": g.sync}
    V, A, PE = g.vector, g.scalar, g.tensor
    listed = [n for q in ORDER for n in ORDER[q]]
    task = {}
    tok = {}

    def near(d):
        a, b = topo.chip(core), topo.chip(T.cores[d])
        return 2 if topo.mates(a, b) else 1 if topo.same_plane(a, b) else 0
    others = sorted([d for d in range(N) if d != r], key=near)
    blocks = others + [r]

    def add(name, deps, fn):
        task[name] = (deps, fn)

    def dma(name, deps, out, in_):
        add(name, deps, lambda q: Q[q].dma_start(out, in_))

    def ts(name, deps, out, in0, s1, op, s2=None, op2=None):
        if op2 is None:
            add(name, deps, lambda q: V.tensor_scalar(out, in0, s1, None, op))
        else:
            add(name, deps, lambda q: V.tensor_scalar(out, in0, s1, s2, op, op2))

    def tt(name, deps, out, in0, in1, op):
        add(name, deps, lambda q: V.tensor_tensor(out, in0, in1, op))

    def copy(name, deps, out, in_):
        add(name, deps, lambda q: V.tensor_copy(out, in_) if q == "v" else A.activation(out, in_, ACT.Copy))

    def fill(name, out, c):
        add(name, [], lambda q: V.memset(out, c) if q == "v" else g.iota(out, [[0, 4 * CN]], 0, 0, allow_small_or_imprecise_dtypes=True))

    def quant(name, deps, c, p, in_):
        add(name, deps, lambda q: V.quantize_mx(c, p, in_))

    def pick(name, deps, out, in_, n, p):
        add(name, deps + seq("wt", range(4)), lambda q: V.tensor_tensor_scan(out[0:p, :], in_[0:p, :], T.wt[0:p, 0:n], 0.0, ALU.max, ALU.mult))

    sent = {"lno": 0, "lme": 0}

    def send(name, deps, ds, lsem, rsem, calls):
        masks = []
        for k, d in enumerate(ds):
            e = topo.engines(core, T.cores[d])
            masks.append(e[k * len(e) // len(ds):(k + 1) * len(e) // len(ds)])
            sent[lsem] += len(calls) * len(masks[-1])

        def fn(q):
            for pairs in calls:
                if len(ds) == 1:
                    rid, pid, _ = topo.addr(T.cores[ds[0]])
                    g.remote_dma(pairs[0][0], pairs[0][1], S[rsem], S[lsem], pid, rid, topo.mask(core, T.cores[ds[0]]))
                else:
                    g.remote_dma_fused([RemoteDMATransfer(dst_ids=[DstId(rid=topo.addr(T.cores[d])[0], pnc=topo.addr(T.cores[d])[1])], dma_engine_mask=sum(1 << e for e in m),
                                                          remote_sem=S[rsem], src=i, dst=o) for d, m, (o, i) in zip(ds, masks, pairs)], local_sem=S[lsem])
        add(name, deps, fn)

    for o, s in enumerate(others):
        n = 2 * len(topo.engines(T.cores[s], core))
        tok["an%d" % s] = ("an%d" % s, n // 2 if (o < 2 and "sendfp" in listed) or (o > 0 and "sendpm" in listed) else n)
        tok["am%d" % s] = ("am%d" % s, n)

    for k in range(2):
        dma("sn.%d" % k, [], T.snl[16 * k:16 * k + 16, :], T.sn[:, :])
        dma("x.%d" % k, [], T.xb[64 * k:64 * k + 64, :], T.x[64 * k:64 * k + 64, :])
    for k in range(8):
        dma("sm.%d" % k, [], T.sml[16 * k:16 * k + 16, :], T.sm[:, 18 * (k // 4):18 * (k // 4) + 18])
    for h in range(2):
        dma("ed.%d" % h, [], T.eds[16 * h:16 * h + 16, 0:31], T.es[:, h:h + 31])
        dma("ed.%d" % (h + 2), [], T.eds[16 * h:16 * h + 16, 32:63], T.ed[:, h:h + 31])
    if "oab" in listed:
        for k in range(8):
            dma("sm.%d" % k, [], T.sml[16 * k:16 * k + 16, :], T.sm[:, 18 * (k // 2 % 2):18 * (k // 2 % 2) + 18])
            dma("ed.%d" % k, [], T.eds[16 * k:16 * k + 16, 0:31], (T.es if k < 4 else T.ed)[:, k % 2:k % 2 + 31])
    dma("wa.0", [], T.wab[:, :], T.wa[:, :])
    dma("wb.0", [], T.wbb[:, :], T.wb[:, :])
    for a in range(4):
        dma("smd.%d" % a, [], T.smd[a:a + 1, :], T.sm[a:16:4, :])
    dma("e.0", ["go"], T.eb[:, :], T.e[:, :])
    dma("v.0", [], T.vb[:, :], T.v[:, :])
    add("go", [], lambda q: g.sem_inc(S.go, 1))
    tok["go"] = ("go", 1)

    add("pi", [], lambda q: g.iota(T.pi[:, :], [[0, 1]], 0, 1))
    add("j4", [], lambda q: g.iota(T.j4[:, :], [[1, 4]], 0, 0, allow_small_or_imprecise_dtypes=True))
    fill("one", T.one[:, :], 1.0)
    fill("pad", T.tr[:, :], 0.0)
    for n, a, b, c in (("win0", 0, WO - 1, 0.0), ("win1", WO - 1, WO, -1e29)):
        if n in ORDER["v"]:
            fill(n, T.win[:, a:b], c)
        else:
            add(n, ["one"], lambda q, a=a, b=b, c=c: A.activation(T.win[:, a:b], T.one[:, a:b], ACT.Identity, scale=c))
    ts("ai", ["pi"], T.ai[:, :], T.pi[:, :], 2, ALU.logical_shift_right, 3, ALU.bitwise_and)
    ts("ii", ["pi"], T.ii[:, :], T.pi[:, :], 3, ALU.bitwise_and)
    copy("af", ["ai"], T.af[:, :], T.ai[:, :])
    copy("ic", ["ii"], T.ic[:, :], T.ii[:, :])
    ts("w1", ["af", "j4"], T.w1[:, :], T.j4[:, :], T.af[:, 0:1], ALU.is_equal, UP, ALU.mult)
    ts("w2", ["af", "j4"], T.w2[:, :], T.j4[:, :], T.af[:, 0:1], ALU.is_gt)
    tt("w4", ["w1", "w2"], T.w4[:, :], T.w1[:, :], T.w2[:, :], ALU.add)
    for m in range(3):
        add("wt%d" % m, ["one", "w4"], lambda q, m=m: A.activation(T.wt[:, m:H:4], T.one[:, :], ACT.Identity, scale=T.w4[:, m:m + 1]))
    fill("tiny", T.tiny[:, :], UP ** -2)
    if "tiny" in listed:
        add("wt3", ["tiny", "w4"], lambda q: A.activation(T.wt[:, 3:H:4], T.tiny[:, :], ACT.Identity, scale=T.w4[:, 3:4]))
    else:
        ts("wt3", ["one", "w4"], T.wt[:, 3:H:4], T.one[:, :], T.w4[:, 3:4], ALU.mult, UP ** -2, ALU.mult)
    hole = 4 * (NT + CN * r)
    fill("holea", T.pa[:, hole:hole + 4 * CN], 0.0)
    fill("holeb", T.pb[:, hole:hole + 4 * CN], 0.0)

    copy("sn1", ["sn.0"], T.snl[32:64, :], T.snl[0:32, :])
    copy("sn2", ["sn1"], T.snl[64:128, :], T.snl[0:64, :])
    for k in range(1, 4):
        copy("sq%d" % k, ["sn.0"], T.snl[32 * k:32 * k + 32, :], T.snl[0:32, :])
    for t in range(4):
        ts("of%d" % t, ["sn2"] if "sn2" in listed else seq("sq", range(1, 4)), T["oft%d" % t][:, :], T.snl[:, :], 4.0, ALU.mult, float(t), ALU.add)
    groups = {"f": others[:1], "p": others[1:2], "d": others[:2], "m": others[2:]}
    assert max(groups["d"]) == min(groups["d"]) + 1
    for x in groups:
        d, n = min(groups[x]), len(groups[x])
        for t in range(4):
            copy("n%s%d" % (x, t), ["x.0", "of%d" % t], T.ht[:, 512 * d + t:512 * (d + n):4], T.xb[:, :].indirect(T["oft%d" % t][:, 8 * d:8 * (d + n)]))
        quant("hq" + x, seq("n" + x, range(4)), T.hq[:, CN * d:CN * (d + n)], T.hp[:, CN * d:CN * (d + n)], T.ht[:, 512 * d:512 * (d + n)])
    there = slice(CN * r, CN * r + CN)
    for x in ("f", "p", "m", "fp", "pm"):
        ds = [groups[c][0] for c in x]
        if "send" + x in listed:
            send("send" + x, ["hq" + c if "hq" + c in listed else "hqd" for c in x], ds, "lno", "an%d" % r,
                 [[(T.nnq[:, there].bitcast(dt.uint8), T.hq[:, CN * c:CN * c + CN].bitcast(dt.uint8)) for c in ds],
                  [(T.nnp[:, there], T.hp[:, CN * c:CN * c + CN]) for c in ds]])

    quant("qa", ["wa.0"], T.waq[:, :], T.wap[:, :], T.wab[:, :])
    quant("qb", ["wb.0"], T.wbq[:, :], T.wbp[:, :], T.wbb[:, :])
    for h in range(2):
        quant("qa%d" % h, ["wa.0"], T.waq[:, 256 * h:256 * h + 256], T.wap[:, 256 * h:256 * h + 256], T.wab[:, 1024 * h:1024 * h + 1024])
        quant("qb%d" % h, ["wb.0"], T.wbq[:, 256 * h:256 * h + 256], T.wbp[:, 256 * h:256 * h + 256], T.wbb[:, 1024 * h:1024 * h + 1024])
    quant("qx", ["x.0"], T.xxq[:, :], T.xxp[:, :], T.xb[:, :])
    quant("qv", ["v.0"], T.vvq[:, :], T.vvp[:, :], T.vb[:, :])

    def product(name, deps, wq, wp, cq, cp, n, out):
        k = ORDER["t"].index(name)
        bank = T.ps[:, 512 * (k % 8):512 * (k % 8) + n]
        add(name, deps + [x.replace("P", "C") for x in ORDER["t"][max(k - 8, 0):max(k - 7, 0)]], lambda q: PE.matmul_mx(bank, wq, wp, cq, cp, True, True))
        copy(name.replace("P", "C"), [name], out, bank)

    pa_full, pb_full = ["holea"], ["holeb"]
    for name in ORDER["t"]:
        j = int(name[2])
        if name[0] == "o":
            deps, cq, cp, h, n = ["qx"], T.xxq[:, :], T.xxp[:, :], 0, NT
        elif name[0] in groups:
            c, n = CN * min(groups[name[0]]), CN * len(groups[name[0]])
            deps, cq, cp, h = seq("an", groups[name[0]]), T.nnq[:, c:c + n], T.nnp[:, c:c + n], NT + c
        else:
            continue
        c, p, w, win, full = (T.waq, T.wap, "qa", T.pa, pa_full) if j < 4 else (T.wbq, T.wbp, "qb", T.pb, pb_full)
        b = slice(128 * (j % 4), 128 * (j % 4) + 128)
        product(name, deps + [w if w in listed else w + str(j % 4 // 2)], c[:, b], p[:, b], cq, cp, n, win[:, 4 * h + j % 4:4 * h + 4 * n:4])
        full.append(name.replace("P", "C"))

    ts("pk0", ["ed.0"], T.pk0[0:32, :], T.eds[0:32, 32:63:2], 8192.0, ALU.mult, 1.0, ALU.add)
    for a in range(4):
        tt("pq%d" % a, ["pk0", "pad"], T.tr[32 * a:32 * a + 32, 0:128:32], T.eds[0:32, 8 * a:8 * a + 7:2], T.pk0[0:32, 4 * a:4 * a + 4], ALU.add)
        add("wn%d" % a, ["trp"], lambda q, a=a: g.partition_broadcast(T.wn[:, 128 * a:128 * a + 128], T.trt[32 * a:32 * a + 1, :], 128))
    add("trp", seq("pq", range(4)), lambda q: V.transpose(T.trt[:, :], T.tr[:, :]))
    tt("pk", ["pk0"], T.pk[0:32, :], T.eds[0:32, 0:31:2], T.pk0[0:32, :], ALU.add)
    copy("pk1", ["pk"], T.pk[32:64, :], T.pk[0:32, :])
    copy("pk2", ["pk1"], T.pk[64:128, :], T.pk[0:64, :])
    add("rp0", [], lambda q: g.iota(T.rpi[:, :], [[1, 16], [0, 2]], 0, 0))
    copy("rp", ["rp0"], T.rp[:, :], T.rpi[:, :])
    copy("wide", ["pk2", "rp"], T.wide[:, :], T.pk[:, :].indirect(T.rp[:, :]))
    add("wn", ["wide"], lambda q: V.transpose(T.wn[:, :], T.wide[:, :]))
    spread = ["wn"] if "wn" in listed else seq("wn", range(4))
    copy("smo", ["sm.0"], T.smo[:, :], T.sml[:, :])
    copy("G", ["smo"] + spread, T.gg[:, :], T.wn[:, :].indirect(T.smo[:, :]))
    pick("scan", ["G"], T.sc, T.gg, H, 128)
    for k in range(2):
        h = blocks[2 * k] // 2
        at = slice(C2 * h, C2 * h + C2)
        for u in range(2):
            ts("ci%d%d" % (k, u), ["scan"], T.ci[64 * u:64 * u + 64, at], T.sc[64 * h:64 * h + 64, 3:H:4], UP, ALU.mult, -1.0, ALU.add)
        both = ["ci%d0" % k, "ci%d1" % k]
        ts("ob%d" % k, both + ["ic"], T.ob[:, at], T.ci[:, at], 1.0 / 2048, ALU.mult, T.ic[:, 0:1], ALU.add)
        ts("cl%d" % k, both, T.cl[:, at], T.ci[:, at], 2047, ALU.bitwise_and)
        ts("oa%d" % k, ["cl%d" % k, "ic"], T.oa[:, at], T.cl[:, at], 4.0, ALU.mult, T.ic[:, 0:1], ALU.add)
    four = ["ci00", "ci01", "ci10", "ci11"]
    ts("ob", four + ["ic"], T.ob[:, :], T.ci[:, :], 1.0 / 2048, ALU.mult, T.ic[:, 0:1], ALU.add)
    ts("cl", four, T.cl[:, :], T.ci[:, :], 2047, ALU.bitwise_and)
    ts("oa", ["cl", "ic"], T.oa[:, :], T.cl[:, :], 4.0, ALU.mult, T.ic[:, 0:1], ALU.add)
    if "oab" in listed:
        add("rp0", [], lambda q: g.iota(T.rpi[:, :], [[2, 16], [0, 2]], 0, 0))
        copy("wide", ["ed.0", "rp"], T.wide[:, :], T.eds[:, 0:31].indirect(T.rp[:, :]))
        add("scan", ["G"] + seq("wt", range(4)), lambda q: V.tensor_tensor_scan(T.sc[:, :], T.gg[:, :], T.wt[:, :], 0.0, ALU.add, ALU.mult))
        for c in range(4):
            ts("o%d" % c, ["scan", "ic"], T.oo[0:32, C2 * c:C2 * c + C2], T.sc[32 * c:32 * c + 32, 3:H:4], 4 * UP, ALU.mult, T.ic[32 * c:32 * c + 32, 0:1], ALU.add)
        copy("oaa", seq("o", range(4)), T.oo[32:64, :], T.oo[0:32, :])
        copy("oab", ["oaa"], T.oo[64:128, :], T.oo[0:64, :])
    add("smr.0", ["smd.0", "ai"] + [n for n in ORDER["g"][:ORDER["g"].index("smr.0")] if n[:2] in ("wn", "ho")], lambda q: g.indirect_dma_start(T.smr[:, :], None, T.smd[:, :], IndirectOffsetOnAxis(ap=T.ai[:, 0:1], axis=0), bounds_check=3))
    oe = seq("oe", range(4))
    for b in range(4):
        add("oe%d" % b, ["smr.0", "ic"], lambda q, out=T.oe[:, b:144:4], in_=T.smr[:, 36 * b:36 * b + 36]:
            A.activation(out, in_, ACT.Identity, bias=T.ic[:, 0:1], scale=4.0) if q == "s" else V.tensor_scalar(out, in_, 4.0, T.ic[:, 0:1], ALU.mult, ALU.add))

    for o, d in enumerate(blocks):
        gb, uu, zz = (T["%s%d" % (n, o)] for n in ("gb", "uu", "zz"))
        c = 36 * d

        def over(step, a, b, o=o):
            return [step + str(o) + x for x in PIECES if step + str(o) + x in listed and PIECES[x][0] < b and a < PIECES[x][1]]
        for x, (a, b) in PIECES.items():
            n, at = str(o) + x, slice(c + a // 16, c + b // 16)
            copy("B" + n, pb_full + ["ob" if "ob" in listed else "ob%d" % (o // 2)], gb[:, a:b], T.pb[:, :].indirect(T.ob[:, at]))
            tt("A" + n, pa_full + ["oa" if "oa" in listed else "oa%d" % (o // 2)] + over("B", a, b), uu[:, a:b], T.pa[:, :].indirect(T.oa[:, at]), gb[:, a:b], ALU.add)
            tt("E" + n, ["e.0"] + oe + over("A", a, b), zz[:, a:b], T.eb[:, :].indirect(T.oe[:, at]), uu[:, a:b], ALU.add)
            if "oab" in listed:
                copy("B" + n, pb_full + ["oab"], gb[:, a:b], T.pb[:, :].indirect(T.oo[:, CM + c + a // 16:CM + c + b // 16]))
                tt("A" + n, pa_full + ["oab"] + over("B", a, b), uu[:, a:b], T.pa[:, :].indirect(T.oo[:, at]), gb[:, a:b], ALU.add)
            copy("F" + n, ["e.0"] + oe, zz[:, a:b], T.eb[:, :].indirect(T.oe[:, at]))
            added = "ac%d.0" % o in listed
            add("R" + n, ["ac%d.0" % o] if added else over("E", a, b), lambda q, out=T.mt[:, W * o + a:W * o + b], in_=(uu if added else zz)[:, a:b]:
                A.activation(out, in_, ACT.Relu, scale=0.05) if q == "s" else V.tensor_scalar(out, in_, 0.0, 0.05, ALU.max, ALU.mult))
        add("ac%d.0" % o, over("A", 0, W) + over("F", 0, W), lambda q, uu=uu, zz=zz: g.dma_start(uu[:, :], zz[:, :], accum_op=ALU.add))
        here, there = slice(CM * o, CM * o + CM), slice(CM * r, CM * r + CM)
        quant("Q%d" % o, over("R", 0, W), T.mmq[:, here], T.mmp[:, here], T.mt[:, W * o:W * o + W])
        if d != r:
            send("send%d" % o, ["Q%d" % o], [d], "lme", "am%d" % r,
                 [[(T.rrq[:, there].bitcast(dt.uint8), T.mmq[:, here].bitcast(dt.uint8))], [(T.rrp[:, there], T.mmp[:, here])]])

    for k in range(8):
        dma("nl.%d" % k, [], T.nlr[4 * k:4 * k + 4, :], T.nl[:, :])
    copy("nl1", ["nl.0"], T.nmv[0:32, :], T.nlr[0:32, :])
    add("nl2", ["nl1" if "nl1" in listed else "nl.0"] + seq("wt", range(4)),
        lambda q: V.tensor_tensor_scan(T.nsc[0:32, :], (T.nmv if "nl1" in listed else T.nlr)[0:32, :], T.wt[0:32, 0:NT], 0.0, ALU.add, ALU.mult))
    tt("nl3", ["nl2"], T.nt1[0:32, :], T.nsc[0:32, 3:128:4], T.nsc[0:32, 131:256:4], ALU.max)
    tt("nl4", ["nl3"], T.nt2[0:32, :], T.nt1[0:32, 0:16], T.nt1[0:32, 16:32], ALU.max)
    ts("nl6", ["nl4"], T.nt3[0:32, :], T.nt2[0:32, :], -0.5 / UP, ALU.is_lt, 1.0 / UP, ALU.mult)
    tt("nl7", ["nl6"], T.nsc[0:32, 3:64:4], T.nsc[0:32, 3:64:4], T.nt3[0:32, :], ALU.subtract)
    for k, (a, b) in enumerate(((0, 32), (32, 64))):
        add("nl%d" % (8 + k), ["nl7"], lambda q, out=T.onl[a:b, :], in_=T.nsc[0:32, 3:256:4]:
            A.activation(out, in_, ACT.Identity, bias=float(WO), scale=UP) if q == "s" else V.tensor_scalar(out, in_, UP, float(WO), ALU.mult, ALU.add))
    copy("on", ["nl8", "nl9"], T.onl[64:128, :], T.onl[0:64, :])
    for k in range(3):
        dma("on.%d" % k, ["nl8"], T.onl[32 * k + 32:32 * k + 64, :], T.onl[0:32, :])

    for n, o in enumerate((0, 1, 3, 2)):
        s = blocks[o]
        if s == r:
            dep, cq, cp = "Q%d" % o, T.mmq[:, CM * o:CM * o + CM], T.mmp[:, CM * o:CM * o + CM]
        else:
            dep, cq, cp = "am%d" % s, T.rrq[:, CM * s:CM * s + CM], T.rrp[:, CM * s:CM * s + CM]
        product("vP%d" % n, ["qv", dep], T.vvq[:, :], T.vvp[:, :], cq, cp, CM, T.win[:, WO + CM * s:WO + CM * s + CM])

    ready = ["win0", "win1", "on" if "on" in listed else "on.0"] + seq("vC", range(4))
    for k, (x, a, b) in enumerate((("a", 0, NA), ("b", NA, NT))):
        steps = (T.g0, T.m1, T.m2, T.yb)
        for f in range(4):
            at = T.win[:, :].indirect(T.onl[:, 16 * f + a // 16:16 * f + b // 16])
            if f == 0:
                copy("y0" + x, ready, T.g0[:, a:b], at)
            else:
                tt("y%d%s" % (f, x), ready + ["y%d%s" % (f - 1, x)], steps[f][:, a:b], at, steps[f - 1][:, a:b], ALU.max)
        dma("y.%d" % k, ["y3" + x], T.y[:, a:b], T.yb[:, a:b])

    silent = ["go"] + [n for n in ORDER["g"] if n.startswith("send")]
    total = {"go": 1}
    total.update(sent)
    for q in ORDER:
        for n in ORDER[q]:
            if n not in silent:
                k, step = ("d_" + n.split(".")[0], 16) if "." in n else ("c" + q, 1)
                total[k] = total.get(k, 0) + step
                tok[n] = (k, total[k])
    for n in list(tok):
        if "." in n:
            tok[n] = (tok[n][0], total[tok[n][0]])
    seen = {}

    def need(q, toks):
        best = {}
        for k, c in toks:
            best[k] = max(best.get(k, 0), c)
        for k in best:
            if seen.get((q, k), 0) < best[k]:
                Q[q].wait_ge(S[k], best[k])
                seen[(q, k)] = best[k]

    for q in ORDER:
        for n in ORDER[q]:
            deps, fn = task[n]
            need(q, [tok[d] for d in deps])
            ins = fn(q)
            if n not in silent:
                ins.then_inc(S[tok[n][0]], 16 if "." in n else 1)
    need("g", list(total.items()) + [tok[n] for n in seq("an", others) + seq("am", others)])
